import numpy as np, ml_dtypes
CORES = [48,51,52,55]
N = 4
import mx_ref
BF = ml_dtypes.bfloat16
def gentries(a):
    return np.ascontiguousarray(a.reshape(8, 16, -1).transpose(0, 2, 1)).reshape(8, -1)
def gtable(e):
    e = np.asarray(e); return np.ascontiguousarray(e.reshape(8, -1, 16).transpose(0, 2, 1)).reshape(128, -1).astype(np.int32)
def gcols(t, e):
    v = np.concatenate([t.reshape(8, 16, -1, 4), np.zeros((8, 16, 1, 4), BF)], axis=2)
    return np.ascontiguousarray(np.stack([v[g][:, e[g]] for g in range(8)])).reshape(128, -1)
def tile(rs):
    return np.stack(rs, axis=2).reshape(128, -1).astype(BF)
def pick(q, e):
    c = np.concatenate([q[0].reshape(128, -1, 4), np.zeros((128, 1, 4), np.uint8)], axis=1); s = np.concatenate([q[1], np.ones((16, 1), np.uint8)], axis=1)
    return (np.ascontiguousarray(c[:, e].reshape(128, -1)), np.ascontiguousarray(s[:, e]))
def join(*qs):
    return (np.concatenate([q[0] for q in qs], axis=1), np.concatenate([q[1] for q in qs], axis=1))
def put(q, e, v):
    c, s = q[0].reshape(128, -1, 4).copy(), q[1].copy(); c[:, e] = v[0].reshape(128, -1, 4); s[:, e] = v[1]
    return (c.reshape(128, -1), s)
def pk(c, s):
    return (np.ascontiguousarray(c), mx_ref.live(s))
def emit(q):
    return q[0], q[1]
def packed(v, rng):
    q = [mx_ref.quantize(np.ascontiguousarray(v[r])) for r in range(N)]
    return np.stack([a for a, b in q]), np.stack([mx_ref.plane(b, rng) for a, b in q])
def values_of_codes():
    e, c = np.zeros((128, 128, 4), np.float32), np.zeros((128, 2, 4), np.uint8)
    e[np.arange(128), np.arange(128), 0] = 1
    c[:127, :, 0] = np.arange(256).reshape(2, 128).T[:127]
    return mx_ref.matmul(mx_ref.quantize(e.reshape(128, 512).astype(BF)), (c.reshape(128, 8), np.full((16, 2), 127, np.uint8))).T.reshape(-1).astype(np.float64)
CODE_VALUE, SCALE_VALUE = values_of_codes(), 2.0 ** (np.arange(256) - 127.0)
def decode(q):
    return (CODE_VALUE[q[0]].reshape(16, 8, -1, 4) * SCALE_VALUE[q[1]][:, None, :, None] + 0.0).reshape(128, -1).astype(np.float32)
def f(rng, *shape):
    return mx_ref.flush((rng.standard_normal(shape, dtype=np.float32) * np.exp2(rng.integers(-2, 3, shape[:-1] + (1,)))).astype(BF))
def wide(rng, *shape, cols=0):
    v = rng.standard_normal(shape, dtype=np.float32) * np.exp2(rng.integers(-12, 13, shape)).astype(np.float32)
    if cols: v *= np.repeat(np.exp2(rng.integers(-cols, cols + 1, shape[:-2] + (1, shape[-1] // 4))) * (rng.random(shape[:-2] + (1, shape[-1] // 4)) > 0.0625), 4, axis=-1).astype(np.float32)
    return mx_ref.flush(v.astype(BF))
C, F = 448, 224
STEP = [1, 2, 3]
def big(v):
    v = v.astype(np.float32)
    v[np.abs(v) < np.float32(2.0 ** -16)] = 0
    return v.astype(BF)
def numbers_of(rng):
    return {"x": big(f(rng, N, 128, 4 * C)), "u": np.array(f(rng, N, 128, 512)), "v": np.array(f(rng, N, 128, 512))}
def stored(q):
    return {k: np.stack([gtable(q[i, r]) for r in range(N)]) for i, k in enumerate(("pl", "dl", "kl"))}
def lists(rng):
    return stored(rng.permuted(np.tile(np.arange(C), (3, N, 8, 1)), axis=3))
def layers(rng):
    return big(f(rng, N, 128, 2048)).reshape(N, 8, 16, 4, 8, 16, 4)
def weights(rng, w):
    c, s = packed(np.ascontiguousarray(w).reshape(N, 128, 2048), rng)
    return {"wc": c, "ws": s}
def deciding(d):
    u = d["u"].reshape(N, 8, 16, 8, 16, 4)
    u[:, :, :, :, :4] = 0
    return u
def setup_inputs(rng):
    return {**numbers_of(rng), **lists(rng), **weights(rng, layers(rng))}
def setup_inputs_ties(rng):
    d = numbers_of(rng)
    o = rng.permutation(N)
    k = rng.integers(-1, 2, (N, 8, C, 4)).astype(np.float32)
    k[o[1]] = 1
    a = np.exp2(rng.integers(-3, 4, 8).astype(np.float32))
    x = d["x"].reshape(N, 8, 16, C, 4)
    x[:, :, 0] = k.astype(BF)
    x[:, :, 4:6] = 0
    x[:, :, 4, :, 0] = 1.96875 * 2.0 ** 5
    x[:, :, 5, :, 0] = 1.125 * 2.0 ** -8
    x[:, :, 8:] = 0
    x[:, :, 8, :, 0] = (-1.125 * a)[None, :, None].astype(BF)
    x[:, :, 10, :, 0] = (-0.0703125 * a)[None, :, None].astype(BF)
    c = np.ones(N, np.float32)
    c[o[0]] = 0
    c[o[2]] = -1
    u = deciding(d)
    w = layers(rng)
    w[:] = 0
    for g in range(8):
        w[:, g, 8, 0, g, 8, 0] = -28.0
        w[:, g, 5, 0, g, 11, 0] = 4.0
        for b in range(4):
            w[:, g, 10, b, g, 9, 0] = -2.0 ** (b - 5)
            u[:, g, 0, g, b, b] = c.astype(BF)
    return {**d, **lists(rng), **weights(rng, w)}
def setup_inputs_near(rng):
    d = numbers_of(rng)
    o = rng.permutation(N) % 4
    x = d["x"].astype(np.float32).reshape(N, 8, 16, C, 4)
    x[:, :, :10] = 0
    u = deciding(d)
    w = layers(rng)
    w[:, :, :10] = 0
    w[:, :, :, :, :, :10] = 0
    for r in range(N):
        k = 2.0 ** -30 if o[r] == 0 else 1.0
        s = rng.integers(-1, 2, (8, C, 4)).astype(np.float64)
        if o[r] == 3:
            x[r] = 0
            x[r, :, 2, :, 0] = 2.0 ** -30
            x[r, :, 7, :, 0] = 2.0 ** -30
            x[r, :, 8] = rng.choice([-1.0, 1.0], (8, C, 4)) * 2.0 ** -29
            x[r, :, 9, :, 0] = 2.0 ** -29
            w[r] = 0
            for g in range(8):
                w[r, g, 7, 0, g, 2, 0] = 32.0
                for b in range(4):
                    w[r, g, 8, b, g, 0, b] = 2.0 ** -10
                    w[r, g, 8, b, g, 1, b] = -2.0 ** -10
                    w[r, g, 0, b, g, 3, b] = 128.0
                    w[r, g, 8, b, g, 5, b] = 2.0 ** -11
                    w[r, g, 0, b, g, 5, b] = 0.5
                    u[r, g, 0, g, b, b] = 1.125 * 2.0 ** -30
                    u[r, g, 1, g, b, b] = 2.0 ** -30
            continue
        if o[r] == 1:
            s *= np.exp2(rng.integers(0, 3, (8, C, 1)).astype(np.float64))
            x[r, :, 0] = 1.125 * s
            x[r, :, 1] = -s
            x[r, :, 7, :, 0] = 1.96875 * 2.0 ** 13
        else:
            x[r, :, 0] = 1.125 * s * k
            x[r, :, 1] = -1.25 * s * k
            x[r, :, 2, :, 0] = k
        for g, j in zip(rng.permutation(8)[:4], [0, C - 1, int(rng.integers(C)), int(rng.integers(C))]): x[r, g, 0, j, 0] = 2.0 ** 30 * rng.choice([-1.0, 1.0])
        for g in range(8):
            for b in range(4):
                u[r, g, 0, g, b, b] = 1.0 if o[r] == 1 else 1.125 * k
                u[r, g, 1, g, b, b] = k
    d["x"] = x.reshape(N, 128, 4 * C).astype(BF)
    return {**d, **lists(rng), **weights(rng, w)}
def setup_inputs_late(rng):
    d = numbers_of(rng)
    o = rng.permutation(N) % 4
    e = np.stack([o & 1, o >> 1, (o + 1) & 1, ((o + 1) >> 1) & 1], axis=1) * 2.0 - 1.0
    d["x"].reshape(N, 8, 16, C, 4)[:, :, 0] = e[:, None, None, :].astype(np.float32).astype(BF)
    u = deciding(d)
    for g in range(8):
        for b in range(4): u[:, g, 0, g, b, b] = 1
    w = layers(rng)
    w[:, :, :, :, :, 0] = (w[:, :, :, :, :, 0].astype(np.float32) * 4).astype(BF)
    return {**d, **lists(rng), **weights(rng, w)}
def setup_inputs_ends(rng):
    d = numbers_of(rng)
    o, e = rng.permutation(N) % 4, rng.permutation(N) % 4
    s = rng.choice([-1.0, 1.0], (N, 128, C, 4))
    s[o == 0] = -1
    s[o == 1] = rng.choice([-1.0, 1.0], (N, 1, C, 1))[o == 1]
    x = s * (0.76 + 0.02 * rng.random((N, 128, C, 4))) * 2.0 ** 30
    x[o == 3] = 2.0 ** -30
    size = np.where(o == 3, 2.0 ** -30, 2.0 ** 30)
    k = np.stack([rng.permutation(8) for r in range(N)])
    a = np.stack([k & 1, (k >> 1) & 1, k >> 2, (k ^ (k >> 1)) & 1], axis=2) * 2.0 - 1.0
    a[k < 2] = 0
    a = a * size[:, None, None]
    deciding(d)[:, :, :, :, :4] = a.astype(np.float32).astype(BF)[:, None, None, :, :, None]
    v = rng.choice([-1.0, 1.0], (N, 128, 512)) * size[:, None, None]
    q = rng.integers(0, C, (3, N, 8, C))
    q[:, e == 0] = C - 1
    q[:, e == 1] = 0
    q[:, e == 1, 7] = C - 1
    q[:, e == 2] = rng.integers(0, 2, (3, 1, 8, C)) * (C - 1)
    w = np.zeros((N, 128, 4, 128, 4), np.float32)
    i = np.arange(128)
    for b in range(4): w[:, i, b, i, b] = np.where(o[:, None] == 3, 128.0, np.where((i >> 4) % 2 == 0, -0.25, 2.0 ** -12)[None, :])
    d["x"] = x.astype(np.float32).reshape(N, 128, 4 * C).astype(BF)
    d["v"] = v.astype(np.float32).astype(BF)
    return {**d, **stored(q), **weights(rng, w.astype(BF))}
def setup_inputs_spread(rng):
    d = setup_inputs(rng)
    d["x"] = big(wide(rng, N, 128, 4 * C, cols=6))
    return d
def check_inputs(d):
    b = []
    for k in ("x", "u", "v"):
        a = np.abs(d[k].astype(np.float32))
        if not (np.isfinite(a).all() and ((a == 0) | (a >= 2.0 ** -30) & (a <= 2.0 ** 30)).all()): b.append("a value of " + k)
    for k in ("pl", "dl", "kl"):
        if not ((d[k] >= 0) & (d[k] < C)).all(): b.append("an entry of " + k)
    none, least, most = [emit(mx_ref.quantize(np.full((128, 16), k, np.float32).astype(BF)))[1][0, 0] for k in (0.0, 2.0 ** -12, 2.0 ** 7)]
    for r in range(N):
        if ((d["wc"][r] == 0x7F) | (d["wc"][r] == 0xFF)).any(): b.append("wc: a code that is no number")
        s = mx_ref.live(d["ws"][r])
        if ((s != none) & ((s < least) | (s > most))).any(): b.append("ws: a scale out of range")
        if (((d["wc"][r].reshape(16, 8, 512, 4) & 0x7F) != 0) & (s == none)[:, None, :, None]).any(): b.append("wc: a code other than zero under the scale of zeros")
    return b
def at(a, e):
    return np.take_along_axis(a, e, axis=1)
def reference(x, u, v, pl, dl, kl, wc, ws):
    qu = [mx_ref.quantize(u[r]) for r in range(N)]
    lay = [pk(wc[r], ws[r]) for r in range(N)]
    drawn = [np.stack([gentries(pl[r]), gentries(dl[r]), gentries(kl[r])]).astype(np.int64) for r in range(N)]
    link = [drawn[r] for r in range(N)]
    now = [x[r] for r in range(N)]
    for step in STEP:
        made = []
        for r in range(N):
            bit = mx_ref.matmul(qu[r], mx_ref.quantize(now[r])).reshape(8, 16, C) > 0
            for j in range(2):
                p, d, k = link[r]
                one, two = at(bit[:, 2 * j], p), at(bit[:, 2 * j + 1], p)
                t = np.where(two, at(p, p), at(d, p))
                there = np.stack([at(p, t), at(d, t), at(k, t)])
                link[r] = np.where(one, there, np.where(two, drawn[r], np.stack([d, k, p])))
            p, d, k = link[r]
            z = ((gcols(now[r], p).astype(np.float32) + gcols(now[r], k).astype(np.float32)) * np.float32(0.5)).astype(BF)
            q = mx_ref.quantize(z)
            made.append(tile([mx_ref.matmul(pick(lay[r], np.arange(128 * b, 128 * b + 128)), q) * np.float32(0.03125) for b in range(4)]))
        new = []
        for r in range(N):
            i = (r - step) % N
            m = at(link[i][2], link[r][0])
            far = gcols(decode(mx_ref.quantize(made[i])).astype(BF), m[:, :F])
            own = gcols(made[r], m[:, F:])
            new.append((now[r].astype(np.float32) + np.concatenate([far, own], axis=1).astype(np.float32)).astype(BF))
        now = new
    y, lk = np.zeros((N, 128, C), np.float32), np.zeros((N, 8, 3 * C), np.float32)
    oc, osc = np.zeros((N, 128, 4 * C), np.uint8), np.zeros((N, 16, C), np.uint8)
    for r in range(N):
        q = mx_ref.quantize(now[r])
        y[r] = mx_ref.matmul(mx_ref.quantize(v[r]), q)
        lk[r] = np.concatenate([link[r][0], link[r][1], link[r][2]], axis=1)
        oc[r], osc[r] = emit(q)
    return {"y": y, "lk": lk, "oc": oc, "osc": osc}

@@ -1,0 +1,517 @@
+from concourse.bass import DstId, RemoteDMATransfer
+from concourse.mybir import dt, AluOpType, ActivationFunctionType
+
+C = 448
+HALF = 224
+U = 448
+CH = 320
+STEP = [1, 2, 3]
+CEN = 224.0
+ROT_A, DRAWN_A = 2, 6
+ROT_B, DRAWN_B = 1, 4
+
+SCRATCH = {
+    "ps": ("psum", [128, 4096], "float32"),
+    "xs": ("sbuf", [128, 4 * C], "bfloat16"),
+    "xh": ("sbuf", [128, 4 * C], "bfloat16"),
+    "tm": ("sbuf", [128, 4 * C], "bfloat16"),
+    "zt": ("sbuf", [128, 4 * C], "bfloat16"),
+    "hb": ("sbuf", [128, 4 * C], "bfloat16"),
+    "hf": ("sbuf", [128, 4 * HALF], "bfloat16"),
+    "qx": ("sbuf", [128, C], "float8_e4m3fn_x4"), "qxs": ("sbuf", [128, C], "uint8"),
+    "qz": ("sbuf", [128, C], "float8_e4m3fn_x4"), "qzs": ("sbuf", [128, C], "uint8"),
+    "ut": ("sbuf", [128, 512], "bfloat16"),
+    "qu": ("sbuf", [128, 128], "float8_e4m3fn_x4"), "qus": ("sbuf", [128, 128], "uint8"),
+    "qr": ("sbuf", [128, 512], "float8_e4m3fn_x4"), "qrs": ("sbuf", [128, 512], "uint8"),
+    "vt": ("sbuf", [128, 512], "bfloat16"),
+    "qv": ("sbuf", [128, 128], "float8_e4m3fn_x4"), "qvs": ("sbuf", [128, 128], "uint8"),
+    "lw": ("sbuf", [128, 512], "float8_e4m3fn_x4"), "lws": ("sbuf", [128, 512], "uint8"),
+    "eb": ("sbuf", [128, 2048], "bfloat16"),
+    "qe": ("sbuf", [128, 512], "float8_e4m3fn_x4"), "qes": ("sbuf", [128, 512], "uint8"),
+    "bwa": ("sbuf", [128, 18 * U], "bfloat16"),
+    "bwb": ("sbuf", [128, 7 * U], "bfloat16"),
+    "sg": ("sbuf", [128, 4 * C], "bfloat16"),
+    "g1": ("sbuf", [128, C], "bfloat16"),
+    "ra": ("sbuf", [128, C], "bfloat16"), "rb": ("sbuf", [128, C], "bfloat16"),
+    "rm": ("sbuf", [128, C], "bfloat16"), "rp": ("sbuf", [128, C], "bfloat16"), "rd": ("sbuf", [128, C], "bfloat16"),
+    "la": ("sbuf", [128, C], "bfloat16"), "lb": ("sbuf", [128, C], "bfloat16"),
+    "l2": ("sbuf", [128, C], "bfloat16"), "l3": ("sbuf", [128, C], "bfloat16"),
+    "lp": ("sbuf", [128, C], "bfloat16"), "lk_": ("sbuf", [128, C], "bfloat16"), "lm_": ("sbuf", [128, C], "bfloat16"),
+    "lpp": ("sbuf", [128, C], "bfloat16"), "ldp": ("sbuf", [128, C], "bfloat16"),
+    "mask": ("sbuf", [128, C], "bfloat16"), "mk2": ("sbuf", [128, C], "bfloat16"),
+    "tt": ("sbuf", [128, C], "float32"),
+    "jj": ("sbuf", [128, 128], "float32"),
+    "pi": ("sbuf", [128, 8], "int32"), "pj": ("sbuf", [128, 8], "int32"),
+    "col": ("sbuf", [128, 8], "float32"),
+    "cq": ("sbuf", [128, 28], "float32"), "q28": ("sbuf", [128, 28], "float32"),
+    "cc": ("sbuf", [128, 28], "float32"), "c2": ("sbuf", [128, 28], "float32"),
+    "ul": ("sbuf", [128, 32], "float32"), "ulu": ("sbuf", [128, 32], "uint16"),
+    "oru": ("sbuf", [128, 28], "uint16"),
+    "hd0": ("sbuf", [128, 168], "float32"), "hd1": ("sbuf", [128, 168], "float32"), "ho": ("sbuf", [128, 168], "float32"),
+    "gd0": ("sbuf", [128, 56], "float32"), "gd1": ("sbuf", [128, 56], "float32"), "go": ("sbuf", [128, 56], "float32"),
+    "ppw": ("sbuf", [128, 28], "float32"), "dpw": ("sbuf", [128, 28], "float32"),
+    "f0": ("sbuf", [128, 28], "uint16"), "f0p": ("sbuf", [128, 28], "uint16"), "f1": ("sbuf", [128, 28], "uint16"),
+    "p1": ("sbuf", [128, 28], "uint16"), "kw": ("sbuf", [128, 28], "uint16"),
+    "pli": ("sbuf", [128, 28], "int32"),
+    "rep": ("sbuf", [128, 3 * C], "int32"),
+    "stage": ("dram", [8, 2, 3, C], "int32"),
+    "ys": ("sbuf", [128, C], "float32"),
+    "lks": ("sbuf", [128, 3 * C], "float32"),
+    "pw0": ("sbuf", [128, 28], "uint16"),
+}
+for _r in (1, 2, 3):
+    SCRATCH["pw%d" % _r] = ("sbuf", [128, 28], "uint16")
+    SCRATCH["pa%d" % _r] = ("sbuf", [128, 28], "uint16")
+    SCRATCH["mw%d" % _r] = ("sbuf", [128, 28], "uint16")
+    SCRATCH["mo%d" % _r] = ("sbuf", [128, 14], "uint16")
+    SCRATCH["qf%d" % _r] = ("sbuf", [128, HALF], "float8_e4m3fn_x4")
+    SCRATCH["qfs%d" % _r] = ("sbuf", [128, HALF], "uint8")
+    SCRATCH["ql%d" % _r] = ("sbuf", [128, HALF], "float8_e4m3fn_x4")
+    SCRATCH["qls%d" % _r] = ("sbuf", [128, HALF], "uint8")
+
+SEMAPHORES = ["eV", "eS", "eT", "eG"] + ["d%d" % i for i in range(60)]
+for _r in (1, 2, 3):
+    SEMAPHORES += ["arrp%d" % _r, "arrm%d" % _r, "arrq%d" % _r, "locp%d" % _r, "locm%d" % _r, "locq%d" % _r]
+
+
+def make_sched(g, T):
+    queues = {"V": g.vector, "S": g.scalar, "T": g.tensor, "G": g, "Y": g.sync}
+    known = {q: {} for q in queues}
+    count = {q: 0 for q in queues}
+    total = {}
+    log = {}
+    ndma = [0]
+
+    def overlap(a, b):
+        if a[1] >= b[2] or b[1] >= a[2]:
+            return False
+        if a[3] > 1 and b[3] > 1 and a[3] == b[3] and a[1] % a[3] != b[1] % b[3]:
+            return False
+        return True
+
+    def covers(a, b):
+        if a[3] == 1:
+            return a[1] <= b[1] and b[2] <= a[2]
+        return a[3] == b[3] and a[1] % a[3] == b[1] % b[3] and a[1] <= b[1] and b[2] <= a[2]
+
+    def wait(q, ev):
+        sem, val, snap = ev
+        if known[q].get(sem, 0) < val:
+            queues[q].wait_ge(T.sem[sem], val)
+            known[q][sem] = val
+            for s, v in snap.items():
+                if known[q].get(s, 0) < v:
+                    known[q][s] = v
+
+    def deps(q, reads, writes, is_async):
+        need = []
+        for reg, w in [(r, r[0] == "ps") for r in reads] + [(r, True) for r in writes]:
+            for (old, ev, oq, oasync, owr) in log.get(reg[0], []):
+                if not overlap(reg, old):
+                    continue
+                if not owr and not w:
+                    continue
+                same = oq == q and not oasync and not is_async
+                if same and not owr:
+                    continue
+                need.append(ev)
+        need.sort(key=lambda e: -e[1])
+        for ev in need:
+            wait(q, ev)
+
+    def note(q, reads, writes, ev, is_async):
+        for reg in reads:
+            log.setdefault(reg[0], []).append((reg, ev, q, is_async, False))
+        for reg in writes:
+            lst = log.setdefault(reg[0], [])
+            lst[:] = [e for e in lst if not covers(reg, e[0])]
+            lst.append((reg, ev, q, is_async, True))
+
+    def op(q, fn, reads, writes):
+        deps(q, reads, writes, False)
+        sem = "e" + q
+        fn().then_inc(T.sem[sem], 1)
+        count[q] += 1
+        total[sem] = count[q]
+        snap = dict(known[q])
+        note(q, reads, writes, (sem, count[q], snap), False)
+
+    def dma(q, out, in_, reads, writes):
+        deps(q, reads, writes, True)
+        sem = "d%d" % ndma[0]
+        ndma[0] += 1
+        queues[q].dma_start(out, in_).then_inc(T.sem[sem], 16)
+        total[sem] = 16
+        note(q, reads, writes, (sem, 16, dict(known[q])), True)
+
+    def remote(fn, reads, loc, n):
+        deps("G", reads, [], True)
+        fn()
+        total[loc] = n
+        note("G", reads, [], (loc, n, dict(known["G"])), True)
+
+    def arrives(writes, sem, n):
+        total[sem] = n
+        note("far", [], writes, (sem, n, {}), True)
+
+    def finish():
+        for sem, v in total.items():
+            if known["G"].get(sem, 0) < v:
+                g.wait_ge(T.sem[sem], v)
+
+    return op, dma, remote, arrives, finish
+
+
+def rank_program(g, core, T, topo):
+    rank = T.rank_of(core)
+    if rank is None:
+        return
+    op, dma, remote, arrives, finish = make_sched(g, T)
+    N = len(T.cores)
+    ALU = AluOpType
+    AF = ActivationFunctionType
+
+    def A(name, a, b, step=1):
+        t = T[name]
+        return (t[:, a:b:step] if step > 1 else t[:, a:b], (name, a, b, step))
+
+    def bank(i, n):
+        return (T.ps[:, 512 * i:512 * i + n], ("ps", 512 * i, 512 * i + 512, 1))
+
+    def IND(win, off, bits=None):
+        w = win[0].bitcast(bits) if bits is not None else win[0]
+        return (w.indirect(off[0]), win[1], off[1])
+
+    def rr(*views):
+        out = []
+        for x in views:
+            if isinstance(x, tuple):
+                out += list(x[1:])
+        return out
+
+    def ap(x):
+        return x[0] if isinstance(x, tuple) else x
+
+    def ts(out, in0, s1, op0, s2=None, op1=None):
+        if op1 is None:
+            op("V", lambda: g.vector.tensor_scalar(ap(out), ap(in0), ap(s1), None, op0), rr(in0, s1), rr(out))
+        else:
+            op("V", lambda: g.vector.tensor_scalar(ap(out), ap(in0), ap(s1), ap(s2), op0, op1), rr(in0, s1, s2), rr(out))
+
+    def tt(out, a, b, o):
+        op("V", lambda: g.vector.tensor_tensor(ap(out), ap(a), ap(b), o), rr(a, b), rr(out))
+
+    def tc(out, a):
+        op("V", lambda: g.vector.tensor_copy(ap(out), ap(a)), rr(a), rr(out))
+
+    def fill(out, val):
+        op("V", lambda: g.vector.memset(ap(out), val), [], rr(out))
+
+    def scan(out, d0, d1):
+        op("V", lambda: g.vector.tensor_tensor_scan(ap(out), ap(d0), ap(d1), 0.0, ALU.mult, ALU.add), rr(d0, d1), rr(out))
+
+    def act(out, a, func=AF.Copy, scale=1.0):
+        if scale == 1.0:
+            op("S", lambda: g.scalar.activation(ap(out), ap(a), func), rr(a), rr(out))
+        else:
+            op("S", lambda: g.scalar.activation(ap(out), ap(a), func, scale=scale), rr(a), rr(out))
+
+    def iota(out, pattern, base, cm):
+        op("G", lambda: g.iota(ap(out), pattern, base, cm, allow_small_or_imprecise_dtypes=True), [], rr(out))
+
+    def quant(codes, plane, tile):
+        op("V", lambda: g.vector.quantize_mx(ap(codes), ap(plane), ap(tile)), rr(tile), rr(codes, plane))
+
+    def mm(out, w, ws, x, xs):
+        op("T", lambda: g.tensor.matmul_mx(ap(out), ap(w), ap(ws), ap(x), ap(xs), True, True), rr(w, ws, x, xs), rr(out))
+
+    def ua(i, n=1):
+        return A("bwa", i * U, (i + n) * U)
+
+    def ub(i, n=1):
+        return A("bwb", i * U, (i + n) * U)
+
+    def wrapped(name):
+        return A(name, 15, C, 16)
+
+    mask = A("mask", 0, C)
+    SC, TH, TG, IF, I28 = [A("col", i, i + 1) for i in range(5)]
+
+    def load_stage(q, l, tin, dup):
+        dma(q, T.stage[:, dup, l, :], tin[:], [], [("stage", 2 * l + dup, 2 * l + dup + 1, 1)])
+
+    dma("S", T.xs[:, 4 * HALF:4 * C], T.x[:, 4 * HALF:4 * C], [], [("xs", 4 * HALF, 4 * C, 1)])
+    dma("S", T.xs[:, 0:4 * HALF], T.x[:, 0:4 * HALF], [], [("xs", 0, 4 * HALF, 1)])
+    load_stage("Y", 0, T.pl, 0)
+    load_stage("Y", 0, T.pl, 1)
+    load_stage("Y", 1, T.dl, 0)
+    load_stage("Y", 1, T.dl, 1)
+    load_stage("Y", 2, T.kl, 0)
+    load_stage("Y", 2, T.kl, 1)
+    dma("Y", T.pli[:], T.pl[:], [], [("pli", 0, 28, 1)])
+    dma("Y", T.ut[:], T.u[:], [], [("ut", 0, 512, 1)])
+    for e in range(8):
+        dma("SY"[e % 2], T.rep[e::8, :], T.stage[:], [("stage", 0, 6, 1)], [("rep%d" % e, 0, 3 * C, 1)])
+    dma("Y", T.lw[:].bitcast(dt.uint8), T.wc[:], [], [("lw", 0, 512, 1)])
+    dma("Y", T.lws[:], T.ws[:], [], [("lws", 0, 512, 1)])
+    dma("Y", T.vt[:], T.v[:], [], [("vt", 0, 512, 1)])
+
+    iota(A("pi", 0, 1), [[1, 1]], 0, 1)
+    iota(A("ul", 0, 32), [[1, 4], [16, 8]], 0, 0)
+    iota(A("tt", 0, C), [[0, 28], [1, 16]], 0, 0)
+    iota(A("cq", 0, 28), [[16, 28]], 0, 0)
+    iota(A("q28", 0, 28), [[1, 28]], 0, 0)
+    iota(A("jj", 0, 128), [[1, 128]], 0, -1)
+    ts(A("pj", 0, 1), A("pi", 0, 1), 15, ALU.bitwise_and)
+    tc(IF, A("pj", 0, 1))
+    ts(I28, IF, 28.0, ALU.mult)
+    ts(A("oru", 0, 28), A("q28", 0, 28), I28, ALU.add)
+    ts(SC, IF, 15.0, ALU.is_equal, 2.0 ** -40, ALU.max)
+    ts(TH, IF, 15.0, ALU.is_lt, 2.0 ** 30, ALU.mult)
+    ts(TH, TH, 0.5, ALU.max)
+    ts(TG, IF, 15.0, ALU.is_lt, 223.5 * 2.0 ** 40, ALU.mult)
+    ts(TG, TG, 223.5, ALU.max)
+    tc(A("ulu", 0, 32), A("ul", 0, 32))
+    ts(A("tt", 0, C), A("tt", 0, C), IF, ALU.subtract)
+    ts(A("mk2", 0, C), A("tt", 0, C), 1.0, ALU.is_equal, 2.0 ** 40, ALU.mult)
+    ts(mask, A("tt", 0, C), 1.0, ALU.is_ge)
+    tt(mask, mask, A("mk2", 0, C), ALU.max)
+    tc(A("pw0", 0, 28), A("pli", 0, 28))
+    ts(A("cc", 0, 28), A("cq", 0, 28), IF, ALU.add)
+    ts(A("c2", 0, 28), A("cc", 0, 28), float(ROT_A * U), ALU.add)
+    fill(A("hd0", 0, 168), 1.0)
+    ts(A("hd0", 0, 168, 6), A("cc", 0, 28), 0.0, ALU.mult)
+    tc(A("hd1", 2, 168, 6), A("c2", 0, 28))
+    ts(A("gd0", 0, 56, 2), A("cc", 0, 28), 0.0, ALU.mult)
+    tc(A("gd1", 0, 56, 2), A("cc", 0, 28))
+    quant(A("qu", 0, 128), A("qus", 0, 128), A("ut", 0, 512))
+    uo = A("ulu", 0, 32)
+    op("V", lambda: g.vector.tensor_copy(T.qr[:, 0:512].bitcast(dt.uint32), T.qu[:, 0:128].bitcast(dt.uint32).indirect(T.ulu[:, 0:32])),
+       [("qu", 0, 128, 1), uo[1]], [("qr", 0, 512, 1)])
+    op("V", lambda: g.vector.tensor_copy(T.qrs[:, 0:512], T.qus[:, 0:128].indirect(T.ulu[:, 0:32])),
+       [("qus", 0, 128, 1), uo[1]], [("qrs", 0, 512, 1)])
+
+    def scores(own):
+        a, b, k = (HALF, C, 0) if own else (0, HALF, 4)
+        quant(A("qx", a, b), A("qxs", a, b), A("xs", 4 * a, 4 * b))
+        for i in range(4):
+            mm(bank(k + i, HALF), A("qr", 128 * i, 128 * i + 128), A("qrs", 128 * i, 128 * i + 128), A("qx", a, b), A("qxs", a, b))
+
+    def sign(i, own, on_vector):
+        a, k = (HALF, 0) if own else (0, 4)
+        out = A("sg", i * C + a, i * C + a + HALF)
+        if on_vector:
+            ts(out, bank(k + i, HALF), 0.0, ALU.is_gt)
+        else:
+            act(out, bank(k + i, HALF), AF.Sign)
+
+    def wrap_own_signs(own):
+        a = HALF if own else 0
+        m = A("mask", a, a + HALF)
+        scan(A("l2", a, a + HALF), m, A("sg", 2 * C + a, 2 * C + a + HALF))
+        scan(A("l3", a, a + HALF), m, A("sg", 3 * C + a, 3 * C + a + HALF))
+
+    def ahead_gather(pw, pu, du):
+        act(A("rp", 0, C), IND(ua(pu), pw))
+        act(A("rd", 0, C), IND(ua(du), pw))
+
+    def ahead_scan():
+        scan(A("lpp", 0, C), mask, A("rp", 0, C))
+        scan(A("ldp", 0, C), mask, A("rd", 0, C))
+        ts(A("ppw", 0, 28), wrapped("lpp"), SC, ALU.mult, CEN - (DRAWN_A - ROT_A) * U, ALU.add)
+        ts(A("dpw", 0, 28), wrapped("ldp"), SC, ALU.mult, CEN, ALU.add)
+        tt(A("hd1", 1, 168, 6), A("dpw", 0, 28), A("c2", 0, 28), ALU.subtract)
+        tt(A("hd1", 0, 168, 6), A("ppw", 0, 28), A("dpw", 0, 28), ALU.subtract)
+
+    def halve(b, own, on_vector):
+        a = HALF if own else 0
+        out, src = A("xh", b * C + a, b * C + a + HALF), A("xs", 4 * a + b, 4 * a + 4 * HALF, 4)
+        if on_vector:
+            ts(out, src, 0.5, ALU.mult)
+        else:
+            act(out, src, AF.Copy, 0.5)
+
+    scores(True)
+    sign(0, True, True)
+    sign(1, True, False)
+    sign(2, True, False)
+    sign(3, True, False)
+    scores(False)
+    sign(0, False, True)
+    sign(1, False, False)
+    sign(2, False, False)
+    sign(3, False, False)
+    reps = [("rep%d" % e, 0, 3 * C, 1) for e in range(8)]
+    for l, u in ((0, DRAWN_A), (1, DRAWN_A + 1), (2, DRAWN_A + 3)):
+        o = ua(u)
+        op("V", lambda: g.vector.tensor_scalar(o[0], T.rep[:, l * C:l * C + C].indirect(T.oru[:, 0:28]), -CEN, None, ALU.add),
+           reps + [("oru", 0, 28, 1)], [o[1]])
+    ahead_gather(A("pw0", 0, 28), DRAWN_A, DRAWN_A + 1)
+    for l in range(3):
+        act(ub(DRAWN_B + l), ua((DRAWN_A, DRAWN_A + 1, DRAWN_A + 3)[l]))
+    for dst, src in ((0, DRAWN_A), (1, DRAWN_A + 1), (2, DRAWN_A + 1), (3, DRAWN_A + 3), (5, DRAWN_A)):
+        tc(ua(dst), ua(src))
+    fill(ua(4), 0.0)
+    fill(ua(8), 0.0)
+    for i in range(10, 18):
+        fill(ua(i), (DRAWN_B if i % 2 == 0 else ROT_B) * U - CEN)
+    wrap_own_signs(True)
+    ahead_scan()
+    for b in range(4):
+        halve(b, True, b < 2)
+        halve(b, False, b < 2)
+    fill(A("eb", 0, 2048), 0.0)
+    for b in range(4):
+        ts(A("eb", 512 * b + b, 512 * b + 512, 4), A("jj", 0, 128), 0.0, ALU.is_equal)
+    quant(A("qe", 0, 512), A("qes", 0, 512), A("eb", 0, 2048))
+
+    for s in STEP:
+        last = s == STEP[-1]
+        src, dst = T.cores[(rank - s) % N], T.cores[(rank + s) % N]
+        pw = A("pw%d" % (s - 1), 0, 28)
+        pn, pa, mw = A("pw%d" % s, 0, 28), A("pa%d" % s, 0, 28), A("mw%d" % s, 0, 28)
+
+        def order(to):
+            e = topo.engines(core, to)
+            return e[::2] + e[1::2]
+
+        def emask(es):
+            m = 0
+            for e in es:
+                m |= 1 << e
+            return m
+
+        tt_gather = IND(A("sg", 0, C), pw)
+        tc(A("ra", 0, C), tt_gather)
+        act(A("rb", 0, C), IND(A("sg", C, 2 * C), pw))
+        if s > 1:
+            sign(2, False, False)
+            sign(3, False, False)
+        scan(A("la", 0, C), mask, A("ra", 0, C))
+        scan(A("lb", 0, C), mask, A("rb", 0, C))
+        ts(A("hd0", 2, 168, 6), wrapped("la"), TH, ALU.is_gt)
+        wrap_own_signs(False)
+        ts(A("hd0", 1, 168, 6), wrapped("lb"), TH, ALU.is_gt)
+        ts(A("hd1", 3, 168, 6), wrapped("lb"), TH, ALU.is_gt, float((DRAWN_A - ROT_A) * U), ALU.mult)
+        ts(A("hd1", 4, 168, 6), wrapped("l2"), TH, ALU.is_le, 10.0 * U, ALU.mult)
+        ts(A("hd1", 5, 168, 6), wrapped("l3"), TH, ALU.is_le, 1.0 * U, ALU.mult)
+        scan(A("ho", 0, 168), A("hd0", 0, 168), A("hd1", 0, 168))
+        tc(A("f0p", 0, 28), A("ho", 5, 168, 6))
+        tc(A("f0", 0, 28), A("ho", 3, 168, 6))
+        f0 = A("f0", 0, 28)
+        tc(ub(0), IND(ua(0, 7), f0))
+        act(A("g1", 0, C), IND(ua(0, 18), A("f0p", 0, 28)))
+        act(ub(1), IND(ua(1, 7), f0))
+        act(ub(2), IND(ua(3, 7), f0))
+        scan(A("lp", 0, C), mask, ub(0))
+        ts(A("p1", 0, 28), wrapped("lp"), SC, ALU.mult, CEN, ALU.add)
+        act(ub(3), ub(0))
+        tc(A("ra", 0, C), IND(A("g1", 0, C), A("p1", 0, 28)))
+        scan(A("la", 0, C), mask, A("ra", 0, C))
+        ts(A("gd0", 1, 56, 2), wrapped("la"), TG, ALU.is_gt)
+        ts(A("gd1", 1, 56, 2), wrapped("la"), SC, ALU.mult, CEN, ALU.add)
+        scan(A("go", 0, 56), A("gd0", 0, 56), A("gd1", 0, 56))
+        f1 = A("f1", 0, 28)
+        tc(f1, A("go", 1, 56, 2))
+        tc(ua(0), IND(ub(0, 5), f1))
+        act(ua(3), IND(ub(2, 5), f1))
+        scan(A("lp", 0, C), mask, ua(0))
+        ts(pn, wrapped("lp"), SC, ALU.mult, CEN, ALU.add)
+        rid, pid, _se = topo.addr(src)
+        m = emask(order(src)[:8])
+        remote(lambda: g.remote_dma(T["pa%d" % s][:], T["pw%d" % s][:], T.sem["arrp%d" % s], T.sem["locp%d" % s], pid, rid, m),
+               [pn[1]], "locp%d" % s, 8)
+        arrives([pa[1]], "arrp%d" % s, 8)
+        kw = A("kw", 0, 28)
+        scan(A("lk_", 0, C), mask, ua(3))
+        ts(kw, wrapped("lk_"), SC, ALU.mult, CEN, ALU.add)
+        for ci, (a, e) in enumerate(((0, CH), (CH, C))):
+            po = A("pw%d" % s, a // 16, e // 16)
+            ko = A("kw", a // 16, e // 16)
+            for b in range(4):
+                act(A("tm", b * C + a, b * C + e), IND(A("xh", b * C, b * C + C), po))
+            for b in range(4):
+                tt(A("zt", 4 * a + b, 4 * e, 4), IND(A("xh", b * C, b * C + C), ko), A("tm", b * C + a, b * C + e), ALU.add)
+            quant(A("qz", a, e), A("qzs", a, e), A("zt", 4 * a, 4 * e))
+            for b in (0, 2, 1, 3):
+                mm(bank(4 * ci + b, e - a), A("lw", 128 * b, 128 * b + 128), A("lws", 128 * b, 128 * b + 128), A("qz", a, e), A("qzs", a, e))
+        act(A("rm", 0, C), IND(ua(3), pa))
+        scan(A("lm_", 0, C), mask, A("rm", 0, C))
+        ts(mw, wrapped("lm_"), SC, ALU.mult, CEN, ALU.add)
+        drid, dpid, _se = topo.addr(dst)
+        md = emask(order(dst)[:8])
+        remote(lambda: g.remote_dma(T["mo%d" % s][:], T["mw%d" % s][:, 14:28], T.sem["arrm%d" % s], T.sem["locm%d" % s], dpid, drid, md),
+               [mw[1]], "locm%d" % s, 8)
+        arrives([("mo%d" % s, 0, 14, 1)], "arrm%d" % s, 8)
+        for ci, (a, e) in enumerate(((0, CH), (CH, C))):
+            for b in (0, 1):
+                act(A("hb", b * C + a, b * C + e), bank(4 * ci + b, e - a), AF.Copy, 0.03125)
+            for b in (2, 3):
+                ts(A("hb", b * C + a, b * C + e), bank(4 * ci + b, e - a), 0.03125, ALU.mult)
+        mf = A("mw%d" % s, 0, 14)
+        for b in (0, 1):
+            act(A("hf", b, 4 * HALF, 4), IND(A("hb", b * C, b * C + C), mf))
+        for b in (2, 3):
+            tc(A("hf", b, 4 * HALF, 4), IND(A("hb", b * C, b * C + C), mf))
+        qf, qfs = "qf%d" % s, "qfs%d" % s
+        quant(A(qf, 0, HALF), A(qfs, 0, HALF), A("hf", 0, 4 * HALF))
+        es = order(dst)
+        trs = []
+        for k in range(4):
+            trs.append((T[qf][:, 56 * k:56 * k + 56].bitcast(dt.uint8), T["ql%d" % s][:, 56 * k:56 * k + 56].bitcast(dt.uint8)))
+        trs.append((T[qfs][:], T["qls%d" % s][:]))
+        calls = [RemoteDMATransfer(dst_ids=[DstId(rid=drid, pnc=dpid)], dma_engine_mask=emask(es[2 * k:2 * k + 2]),
+                                   remote_sem=T.sem["arrq%d" % s], src=a, dst=b) for k, (a, b) in enumerate(trs)]
+        remote(lambda: g.remote_dma_fused(calls, local_sem=T.sem["locq%d" % s]), [(qf, 0, HALF, 1), (qfs, 0, HALF, 1)], "locq%d" % s, 10)
+        arrives([("ql%d" % s, 0, HALF, 1), ("qls%d" % s, 0, HALF, 1)], "arrq%d" % s, 10)
+        act(ua(1), IND(ub(1, 5), f1))
+        if not last:
+            ahead_gather(pn, 0, 1)
+        mo = A("mo%d" % s, 0, 14)
+        for b in range(4):
+            x = A("xs", 4 * HALF + b, 4 * C, 4)
+            tt(x, IND(A("hb", b * C, b * C + C), mo), x, ALU.add)
+        if not last:
+            scores(True)
+            tc(ua(2), ua(1))
+            ahead_scan()
+            sign(0, True, True)
+            for i in (1, 2, 3):
+                sign(i, True, False)
+            tc(ua(5), ua(0))
+            wrap_own_signs(True)
+            for b in range(4):
+                halve(b, True, True)
+        else:
+            quant(A("qv", 0, 128), A("qvs", 0, 128), A("vt", 0, 512))
+            quant(A("qx", HALF, C), A("qxs", HALF, C), A("xs", 4 * HALF, 4 * C))
+            mm(bank(0, HALF), A("qv", 0, 128), A("qvs", 0, 128), A("qx", HALF, C), A("qxs", HALF, C))
+            for l, u in ((0, 0), (1, 1), (2, 3)):
+                ts(A("lks", l * C, l * C + C), ua(u), CEN, ALU.add)
+            act(A("ys", HALF, C), bank(0, HALF))
+            dma("Y", T.oc[:, 4 * HALF:4 * C], T.qx[:, HALF:C].bitcast(dt.uint8), [("qx", HALF, C, 1)], [])
+            for k in range(4):
+                dma("Y", T.osc[4 * k:4 * k + 4, HALF:C], T.qxs[32 * k:32 * k + 4, HALF:C], [("qxs", HALF, C, 1)], [])
+            dma("Y", T.lk[:], T.lks[0::16, :], [("lks", 0, 3 * C, 1)], [])
+            dma("Y", T.y[:, HALF:C], T.ys[:, HALF:C], [("ys", HALF, C, 1)], [])
+        for b in range(4):
+            mm(bank(4 + b, HALF), A("qe", 128 * b, 128 * b + 128), A("qes", 128 * b, 128 * b + 128),
+               A("ql%d" % s, 0, HALF), A("qls%d" % s, 0, HALF))
+        for b in range(4):
+            x = A("xs", b, 4 * HALF, 4)
+            tt(x, bank(4 + b, HALF), x, ALU.add)
+            if not last:
+                halve(b, False, False)
+        if not last:
+            scores(False)
+            sign(0, False, True)
+            sign(1, False, False)
+        else:
+            quant(A("qx", 0, HALF), A("qxs", 0, HALF), A("xs", 0, 4 * HALF))
+            mm(bank(1, HALF), A("qv", 0, 128), A("qvs", 0, 128), A("qx", 0, HALF), A("qxs", 0, HALF))
+            dma("Y", T.oc[:, 0:4 * HALF], T.qx[:, 0:HALF].bitcast(dt.uint8), [("qx", 0, HALF, 1)], [])
+            for k in range(4):
+                dma("YS"[k % 2], T.osc[4 * k:4 * k + 4, 0:HALF], T.qxs[32 * k:32 * k + 4, 0:HALF], [("qxs", 0, HALF, 1)], [])
+            tc(A("ys", 0, HALF), bank(1, HALF))
+            dma("S", T.y[:, 0:HALF], T.ys[:, 0:HALF], [("ys", 0, HALF, 1)], [])
+    finish()

@@ -39,7 +39,7 @@ SCRATCH = {
     "lp": ("sbuf", [128, C], "bfloat16"), "lk_": ("sbuf", [128, C], "bfloat16"), "lm_": ("sbuf", [128, C], "bfloat16"),
     "lpp": ("sbuf", [128, C], "bfloat16"), "ldp": ("sbuf", [128, C], "bfloat16"),
     "mask": ("sbuf", [128, C], "bfloat16"), "mk2": ("sbuf", [128, C], "bfloat16"),
-    "tt": ("sbuf", [128, C], "float32"),
+    "tt": ("sbuf", [128, C], "bfloat16"),
     "jj": ("sbuf", [128, 128], "float32"),
     "pi": ("sbuf", [128, 8], "int32"), "pj": ("sbuf", [128, 8], "int32"),
     "col": ("sbuf", [128, 8], "float32"),
@@ -107,12 +107,9 @@ def make_sched(g, T):
         need = []
         for reg, w in [(r, r[0] == "ps") for r in reads] + [(r, True) for r in writes]:
             for (old, ev, oq, oasync, owr) in log.get(reg[0], []):
-                if not overlap(reg, old):
+                if not overlap(reg, old) or not (owr or w):
                     continue
-                if not owr and not w:
-                    continue
-                same = oq == q and not oasync and not is_async
-                if same and not owr:
+                if oq == q and not oasync and not is_async and not owr:
                     continue
                 need.append(ev)
         need.sort(key=lambda e: -e[1])
@@ -133,8 +130,7 @@ def make_sched(g, T):
         fn().then_inc(T.sem[sem], 1)
         count[q] += 1
         total[sem] = count[q]
-        snap = dict(known[q])
-        note(q, reads, writes, (sem, count[q], snap), False)
+        note(q, reads, writes, (sem, count[q], dict(known[q])), False)
 
     def dma(q, out, in_, reads, writes):
         deps(q, reads, writes, True)
@@ -178,9 +174,8 @@ def rank_program(g, core, T, topo):
     def bank(i, n):
         return (T.ps[:, 512 * i:512 * i + n], ("ps", 512 * i, 512 * i + 512, 1))
 
-    def IND(win, off, bits=None):
-        w = win[0].bitcast(bits) if bits is not None else win[0]
-        return (w.indirect(off[0]), win[1], off[1])
+    def IND(win, off):
+        return (win[0].indirect(off[0]), win[1], off[1])
 
     def rr(*views):
         out = []
@@ -235,21 +230,18 @@ def rank_program(g, core, T, topo):
         return A(name, 15, C, 16)
 
     mask = A("mask", 0, C)
-    SC, TH, TG, IF, I28 = [A("col", i, i + 1) for i in range(5)]
+    SC, TH, TG, IF, I28, IF1 = [A("col", i, i + 1) for i in range(6)]
 
     def load_stage(q, l, tin, dup):
         dma(q, T.stage[:, dup, l, :], tin[:], [], [("stage", 2 * l + dup, 2 * l + dup + 1, 1)])
 
     dma("S", T.xs[:, 4 * HALF:4 * C], T.x[:, 4 * HALF:4 * C], [], [("xs", 4 * HALF, 4 * C, 1)])
     dma("S", T.xs[:, 0:4 * HALF], T.x[:, 0:4 * HALF], [], [("xs", 0, 4 * HALF, 1)])
-    load_stage("Y", 0, T.pl, 0)
-    load_stage("Y", 0, T.pl, 1)
-    load_stage("Y", 1, T.dl, 0)
-    load_stage("Y", 1, T.dl, 1)
-    load_stage("Y", 2, T.kl, 0)
-    load_stage("Y", 2, T.kl, 1)
-    dma("Y", T.pli[:], T.pl[:], [], [("pli", 0, 28, 1)])
     dma("Y", T.ut[:], T.u[:], [], [("ut", 0, 512, 1)])
+    dma("Y", T.pli[:], T.pl[:], [], [("pli", 0, 28, 1)])
+    for l, tin in ((0, T.pl), (1, T.dl), (2, T.kl)):
+        load_stage("Y", l, tin, 0)
+        load_stage("S", l, tin, 1)
     for e in range(8):
         dma("SY"[e % 2], T.rep[e::8, :], T.stage[:], [("stage", 0, 6, 1)], [("rep%d" % e, 0, 3 * C, 1)])
     dma("Y", T.lw[:].bitcast(dt.uint8), T.wc[:], [], [("lw", 0, 512, 1)])
@@ -259,36 +251,32 @@ def rank_program(g, core, T, topo):
     iota(A("pi", 0, 1), [[1, 1]], 0, 1)
     iota(A("ul", 0, 32), [[1, 4], [16, 8]], 0, 0)
     iota(A("tt", 0, C), [[0, 28], [1, 16]], 0, 0)
-    iota(A("cq", 0, 28), [[16, 28]], 0, 0)
     iota(A("q28", 0, 28), [[1, 28]], 0, 0)
+    iota(A("cq", 0, 28), [[16, 28]], 0, 0)
     iota(A("jj", 0, 128), [[1, 128]], 0, -1)
+    iota(ua(10, 8), [[0, 4], [(ROT_B - DRAWN_B) * U, 2], [0, U]], DRAWN_B * U - int(CEN), 0)
+    fill(A("eb", 0, 1024), 0.0)
+    act(A("eb", 1024, 2048), A("eb", 0, 1024))
     ts(A("pj", 0, 1), A("pi", 0, 1), 15, ALU.bitwise_and)
     tc(IF, A("pj", 0, 1))
+    tc(A("ulu", 0, 32), A("ul", 0, 32))
+    ts(IF1, IF, 1.0, ALU.add)
     ts(I28, IF, 28.0, ALU.mult)
-    ts(A("oru", 0, 28), A("q28", 0, 28), I28, ALU.add)
     ts(SC, IF, 15.0, ALU.is_equal, 2.0 ** -40, ALU.max)
     ts(TH, IF, 15.0, ALU.is_lt, 2.0 ** 30, ALU.mult)
-    ts(TH, TH, 0.5, ALU.max)
     ts(TG, IF, 15.0, ALU.is_lt, 223.5 * 2.0 ** 40, ALU.mult)
+    ts(TH, TH, 0.5, ALU.max)
     ts(TG, TG, 223.5, ALU.max)
-    tc(A("ulu", 0, 32), A("ul", 0, 32))
-    ts(A("tt", 0, C), A("tt", 0, C), IF, ALU.subtract)
-    ts(A("mk2", 0, C), A("tt", 0, C), 1.0, ALU.is_equal, 2.0 ** 40, ALU.mult)
-    ts(mask, A("tt", 0, C), 1.0, ALU.is_ge)
+    ts(A("mk2", 0, C), A("tt", 0, C), IF1, ALU.is_equal, 2.0 ** 40, ALU.mult)
+    ts(mask, A("tt", 0, C), IF1, ALU.is_ge)
+    ts(A("oru", 0, 28), A("q28", 0, 28), I28, ALU.add)
     tt(mask, mask, A("mk2", 0, C), ALU.max)
-    tc(A("pw0", 0, 28), A("pli", 0, 28))
     ts(A("cc", 0, 28), A("cq", 0, 28), IF, ALU.add)
-    ts(A("c2", 0, 28), A("cc", 0, 28), float(ROT_A * U), ALU.add)
-    fill(A("hd0", 0, 168), 1.0)
-    ts(A("hd0", 0, 168, 6), A("cc", 0, 28), 0.0, ALU.mult)
-    tc(A("hd1", 2, 168, 6), A("c2", 0, 28))
-    ts(A("gd0", 0, 56, 2), A("cc", 0, 28), 0.0, ALU.mult)
-    tc(A("gd1", 0, 56, 2), A("cc", 0, 28))
     quant(A("qu", 0, 128), A("qus", 0, 128), A("ut", 0, 512))
     uo = A("ulu", 0, 32)
     op("V", lambda: g.vector.tensor_copy(T.qr[:, 0:512].bitcast(dt.uint32), T.qu[:, 0:128].bitcast(dt.uint32).indirect(T.ulu[:, 0:32])),
        [("qu", 0, 128, 1), uo[1]], [("qr", 0, 512, 1)])
-    op("V", lambda: g.vector.tensor_copy(T.qrs[:, 0:512], T.qus[:, 0:128].indirect(T.ulu[:, 0:32])),
+    op("S", lambda: g.scalar.activation(T.qrs[:, 0:512], T.qus[:, 0:128].indirect(T.ulu[:, 0:32]), AF.Copy),
        [("qus", 0, 128, 1), uo[1]], [("qrs", 0, 512, 1)])
 
     def scores(own):
@@ -305,11 +293,15 @@ def rank_program(g, core, T, topo):
         else:
             act(out, bank(k + i, HALF), AF.Sign)
 
-    def wrap_own_signs(own):
+    def wrap_signs(own):
         a = HALF if own else 0
         m = A("mask", a, a + HALF)
         scan(A("l2", a, a + HALF), m, A("sg", 2 * C + a, 2 * C + a + HALF))
         scan(A("l3", a, a + HALF), m, A("sg", 3 * C + a, 3 * C + a + HALF))
+
+    def look_up_signs(pw):
+        tc(A("ra", 0, C), IND(A("sg", 0, C), pw))
+        act(A("rb", 0, C), IND(A("sg", C, 2 * C), pw))
 
     def ahead_gather(pw, pu, du):
         act(A("rp", 0, C), IND(ua(pu), pw))
@@ -331,39 +323,57 @@ def rank_program(g, core, T, topo):
         else:
             act(out, src, AF.Copy, 0.5)
 
+    def copy_unit(dst, src):
+        dma("Y", dst[0], src[0], [src[1]], [dst[1]])
+
+    def order(to):
+        e = topo.engines(core, to)
+        return e[::2] + e[1::2]
+
+    def emask(es):
+        m = 0
+        for e in es:
+            m |= 1 << e
+        return m
+
+    pw0 = A("pw0", 0, 28)
     scores(True)
-    sign(0, True, True)
-    sign(1, True, False)
-    sign(2, True, False)
-    sign(3, True, False)
     scores(False)
-    sign(0, False, True)
+    sign(1, True, False)
     sign(1, False, False)
-    sign(2, False, False)
-    sign(3, False, False)
     reps = [("rep%d" % e, 0, 3 * C, 1) for e in range(8)]
-    for l, u in ((0, DRAWN_A), (1, DRAWN_A + 1), (2, DRAWN_A + 3)):
-        o = ua(u)
+
+    def drawn(l):
+        o = ua((DRAWN_A, DRAWN_A + 1, DRAWN_A + 3)[l])
         op("V", lambda: g.vector.tensor_scalar(o[0], T.rep[:, l * C:l * C + C].indirect(T.oru[:, 0:28]), -CEN, None, ALU.add),
            reps + [("oru", 0, 28, 1)], [o[1]])
-    ahead_gather(A("pw0", 0, 28), DRAWN_A, DRAWN_A + 1)
-    for l in range(3):
-        act(ub(DRAWN_B + l), ua((DRAWN_A, DRAWN_A + 1, DRAWN_A + 3)[l]))
-    for dst, src in ((0, DRAWN_A), (1, DRAWN_A + 1), (2, DRAWN_A + 1), (3, DRAWN_A + 3), (5, DRAWN_A)):
-        tc(ua(dst), ua(src))
-    fill(ua(4), 0.0)
-    fill(ua(8), 0.0)
-    for i in range(10, 18):
-        fill(ua(i), (DRAWN_B if i % 2 == 0 else ROT_B) * U - CEN)
-    wrap_own_signs(True)
-    ahead_scan()
+        for dst in ((ua(0), ua(5), ub(DRAWN_B)), (ua(1), ua(2), ub(DRAWN_B + 1)), (ua(3), ub(DRAWN_B + 2)))[l]:
+            copy_unit(dst, o)
+
+    tc(pw0, A("pli", 0, 28))
+    fill(A("hd0", 0, 168), 1.0)
+    ts(A("c2", 0, 28), A("cc", 0, 28), float(ROT_A * U), ALU.add)
+    ts(A("gd0", 0, 56, 2), A("cc", 0, 28), 0.0, ALU.mult)
+    tc(A("gd1", 0, 56, 2), A("cc", 0, 28))
+    ts(A("hd0", 0, 168, 6), A("cc", 0, 28), 0.0, ALU.mult)
+    tc(A("hd1", 2, 168, 6), A("c2", 0, 28))
+    drawn(0)
+    drawn(1)
+    sign(0, True, True)
+    sign(0, False, True)
+    ahead_gather(pw0, DRAWN_A, DRAWN_A + 1)
+    look_up_signs(pw0)
+    for own in (True, False):
+        sign(2, own, False)
+        sign(3, own, False)
+    drawn(2)
     for b in range(4):
         halve(b, True, b < 2)
         halve(b, False, b < 2)
-    fill(A("eb", 0, 2048), 0.0)
-    for b in range(4):
-        ts(A("eb", 512 * b + b, 512 * b + 512, 4), A("jj", 0, 128), 0.0, ALU.is_equal)
-    quant(A("qe", 0, 512), A("qes", 0, 512), A("eb", 0, 2048))
+    fill(ua(4), 0.0)
+    fill(ua(8), 0.0)
+    ahead_scan()
+    wrap_signs(True)
 
     for s in STEP:
         last = s == STEP[-1]
@@ -371,26 +381,17 @@ def rank_program(g, core, T, topo):
         pw = A("pw%d" % (s - 1), 0, 28)
         pn, pa, mw = A("pw%d" % s, 0, 28), A("pa%d" % s, 0, 28), A("mw%d" % s, 0, 28)
 
-        def order(to):
-            e = topo.engines(core, to)
-            return e[::2] + e[1::2]
-
-        def emask(es):
-            m = 0
-            for e in es:
-                m |= 1 << e
-            return m
-
-        tt_gather = IND(A("sg", 0, C), pw)
-        tc(A("ra", 0, C), tt_gather)
-        act(A("rb", 0, C), IND(A("sg", C, 2 * C), pw))
         if s > 1:
+            look_up_signs(pw)
             sign(2, False, False)
             sign(3, False, False)
         scan(A("la", 0, C), mask, A("ra", 0, C))
         scan(A("lb", 0, C), mask, A("rb", 0, C))
+        if s > 1:
+            for b in range(4):
+                halve(b, True, False)
         ts(A("hd0", 2, 168, 6), wrapped("la"), TH, ALU.is_gt)
-        wrap_own_signs(False)
+        wrap_signs(False)
         ts(A("hd0", 1, 168, 6), wrapped("lb"), TH, ALU.is_gt)
         ts(A("hd1", 3, 168, 6), wrapped("lb"), TH, ALU.is_gt, float((DRAWN_A - ROT_A) * U), ALU.mult)
         ts(A("hd1", 4, 168, 6), wrapped("l2"), TH, ALU.is_le, 10.0 * U, ALU.mult)
@@ -435,6 +436,9 @@ def rank_program(g, core, T, topo):
             quant(A("qz", a, e), A("qzs", a, e), A("zt", 4 * a, 4 * e))
             for b in (0, 2, 1, 3):
                 mm(bank(4 * ci + b, e - a), A("lw", 128 * b, 128 * b + 128), A("lws", 128 * b, 128 * b + 128), A("qz", a, e), A("qzs", a, e))
+        if s == 1:
+            for b in range(4):
+                ts(A("eb", 512 * b + b, 512 * b + 512, 4), A("jj", 0, 128), 0.0, ALU.is_equal)
         act(A("rm", 0, C), IND(ua(3), pa))
         scan(A("lm_", 0, C), mask, A("rm", 0, C))
         ts(mw, wrapped("lm_"), SC, ALU.mult, CEN, ALU.add)
@@ -444,9 +448,9 @@ def rank_program(g, core, T, topo):
                [mw[1]], "locm%d" % s, 8)
         arrives([("mo%d" % s, 0, 14, 1)], "arrm%d" % s, 8)
         for ci, (a, e) in enumerate(((0, CH), (CH, C))):
-            for b in (0, 1):
+            for b in ((0, 1), (2, 3, 0, 1))[ci]:
                 act(A("hb", b * C + a, b * C + e), bank(4 * ci + b, e - a), AF.Copy, 0.03125)
-            for b in (2, 3):
+            for b in ((2, 3), ())[ci]:
                 ts(A("hb", b * C + a, b * C + e), bank(4 * ci + b, e - a), 0.03125, ALU.mult)
         mf = A("mw%d" % s, 0, 14)
         for b in (0, 1):
@@ -471,17 +475,17 @@ def rank_program(g, core, T, topo):
         for b in range(4):
             x = A("xs", 4 * HALF + b, 4 * C, 4)
             tt(x, IND(A("hb", b * C, b * C + C), mo), x, ALU.add)
+        if s == 1:
+            quant(A("qe", 0, 512), A("qes", 0, 512), A("eb", 0, 2048))
         if not last:
             scores(True)
-            tc(ua(2), ua(1))
+            copy_unit(ua(5), ua(0))
+            copy_unit(ua(2), ua(1))
             ahead_scan()
             sign(0, True, True)
             for i in (1, 2, 3):
                 sign(i, True, False)
-            tc(ua(5), ua(0))
-            wrap_own_signs(True)
-            for b in range(4):
-                halve(b, True, True)
+            wrap_signs(True)
         else:
             quant(A("qv", 0, 128), A("qvs", 0, 128), A("vt", 0, 512))
             quant(A("qx", HALF, C), A("qxs", HALF, C), A("xs", 4 * HALF, 4 * C))

@@ -1,14 +1,16 @@
-from concourse.bass import DstId, RemoteDMATransfer
 from concourse.mybir import dt, AluOpType, ActivationFunctionType
 
 C = 448
 HALF = 224
 U = 448
-CH = 320
+CH = 288
 STEP = [1, 2, 3]
 CEN = 224.0
 ROT_A, DRAWN_A = 2, 6
-ROT_B, DRAWN_B = 1, 4
+ROT_B, DRAWN_B = 1, 3
+TO = ((0, 2, 1, 3), (0, 2, 1, 3))
+EVS, EVV = ((0, 2, 1), (0, 1)), ((3,), (2, 3))
+SPL = 22
 
 SCRATCH = {
     "ps": ("psum", [128, 4096], "float32"),
@@ -29,7 +31,7 @@ SCRATCH = {
     "eb": ("sbuf", [128, 2048], "bfloat16"),
     "qe": ("sbuf", [128, 512], "float8_e4m3fn_x4"), "qes": ("sbuf", [128, 512], "uint8"),
     "bwa": ("sbuf", [128, 18 * U], "bfloat16"),
-    "bwb": ("sbuf", [128, 7 * U], "bfloat16"),
+    "bwb": ("sbuf", [128, 9 * U], "bfloat16"),
     "sg": ("sbuf", [128, 4 * C], "bfloat16"),
     "g1": ("sbuf", [128, C], "bfloat16"),
     "ra": ("sbuf", [128, C], "bfloat16"), "rb": ("sbuf", [128, C], "bfloat16"),
@@ -71,7 +73,8 @@ for _r in (1, 2, 3):
 
 SEMAPHORES = ["eV", "eS", "eT", "eG"] + ["d%d" % i for i in range(60)]
 for _r in (1, 2, 3):
-    SEMAPHORES += ["arrp%d" % _r, "arrm%d" % _r, "arrq%d" % _r, "locp%d" % _r, "locm%d" % _r, "locq%d" % _r]
+    for _k in "pmqs":
+        SEMAPHORES += ["arr%s%d" % (_k, _r), "loc%s%d" % (_k, _r)]
 
 
 def make_sched(g, T):
@@ -205,8 +208,10 @@ def rank_program(g, core, T, topo):
     def scan(out, d0, d1):
         op("V", lambda: g.vector.tensor_tensor_scan(ap(out), ap(d0), ap(d1), 0.0, ALU.mult, ALU.add), rr(d0, d1), rr(out))
 
-    def act(out, a, func=AF.Copy, scale=1.0):
-        if scale == 1.0:
+    def act(out, a, func=AF.Copy, scale=1.0, bias=None):
+        if bias is not None:
+            op("S", lambda: g.scalar.activation(ap(out), ap(a), func, bias=bias, scale=scale), rr(a), rr(out))
+        elif scale == 1.0:
             op("S", lambda: g.scalar.activation(ap(out), ap(a), func), rr(a), rr(out))
         else:
             op("S", lambda: g.scalar.activation(ap(out), ap(a), func, scale=scale), rr(a), rr(out))
@@ -243,7 +248,7 @@ def rank_program(g, core, T, topo):
         load_stage("Y", l, tin, 0)
         load_stage("S", l, tin, 1)
     for e in range(8):
-        dma("SY"[e % 2], T.rep[e::8, :], T.stage[:], [("stage", 0, 6, 1)], [("rep%d" % e, 0, 3 * C, 1)])
+        dma("Y", T.rep[e::8, :], T.stage[:], [("stage", 0, 6, 1)], [("rep%d" % e, 0, 3 * C, 1)])
     dma("Y", T.lw[:].bitcast(dt.uint8), T.wc[:], [], [("lw", 0, 512, 1)])
     dma("Y", T.lws[:], T.ws[:], [], [("lws", 0, 512, 1)])
     dma("Y", T.vt[:], T.v[:], [], [("vt", 0, 512, 1)])
@@ -251,12 +256,15 @@ def rank_program(g, core, T, topo):
     iota(A("pi", 0, 1), [[1, 1]], 0, 1)
     iota(A("ul", 0, 32), [[1, 4], [16, 8]], 0, 0)
     iota(A("tt", 0, C), [[0, 28], [1, 16]], 0, 0)
+    iota(A("jj", 0, 128), [[1, 128]], 0, -1)
     iota(A("q28", 0, 28), [[1, 28]], 0, 0)
     iota(A("cq", 0, 28), [[16, 28]], 0, 0)
-    iota(A("jj", 0, 128), [[1, 128]], 0, -1)
     iota(ua(10, 8), [[0, 4], [(ROT_B - DRAWN_B) * U, 2], [0, U]], DRAWN_B * U - int(CEN), 0)
     fill(A("eb", 0, 1024), 0.0)
     act(A("eb", 1024, 2048), A("eb", 0, 1024))
+    act(A("jj", 0, 128), A("jj", 0, 128), AF.Abs)
+    for b in range(4):
+        act(A("eb", 512 * b + b, 512 * b + 512, 4), A("jj", 0, 128), AF.Relu, -1.0, 1.0)
     ts(A("pj", 0, 1), A("pi", 0, 1), 15, ALU.bitwise_and)
     tc(IF, A("pj", 0, 1))
     tc(A("ulu", 0, 32), A("ul", 0, 32))
@@ -279,10 +287,11 @@ def rank_program(g, core, T, topo):
     op("S", lambda: g.scalar.activation(T.qrs[:, 0:512], T.qus[:, 0:128].indirect(T.ulu[:, 0:32]), AF.Copy),
        [("qus", 0, 128, 1), uo[1]], [("qrs", 0, 512, 1)])
 
-    def scores(own):
+    def scores(own, bits, q=True):
         a, b, k = (HALF, C, 0) if own else (0, HALF, 4)
-        quant(A("qx", a, b), A("qxs", a, b), A("xs", 4 * a, 4 * b))
-        for i in range(4):
+        if q:
+            quant(A("qx", a, b), A("qxs", a, b), A("xs", 4 * a, 4 * b))
+        for i in bits:
             mm(bank(k + i, HALF), A("qr", 128 * i, 128 * i + 128), A("qrs", 128 * i, 128 * i + 128), A("qx", a, b), A("qxs", a, b))
 
     def sign(i, own, on_vector):
@@ -315,13 +324,9 @@ def rank_program(g, core, T, topo):
         tt(A("hd1", 1, 168, 6), A("dpw", 0, 28), A("c2", 0, 28), ALU.subtract)
         tt(A("hd1", 0, 168, 6), A("ppw", 0, 28), A("dpw", 0, 28), ALU.subtract)
 
-    def halve(b, own, on_vector):
+    def halve(b, own):
         a = HALF if own else 0
-        out, src = A("xh", b * C + a, b * C + a + HALF), A("xs", 4 * a + b, 4 * a + 4 * HALF, 4)
-        if on_vector:
-            ts(out, src, 0.5, ALU.mult)
-        else:
-            act(out, src, AF.Copy, 0.5)
+        act(A("xh", b * C + a, b * C + a + HALF), A("xs", 4 * a + b, 4 * a + 4 * HALF, 4), AF.Copy, 0.5)
 
     def copy_unit(dst, src):
         dma("Y", dst[0], src[0], [src[1]], [dst[1]])
@@ -337,8 +342,10 @@ def rank_program(g, core, T, topo):
         return m
 
     pw0 = A("pw0", 0, 28)
-    scores(True)
-    scores(False)
+    scores(True, (2, 3, 0, 1))
+    scores(False, (0, 1, 2, 3))
+    sign(2, True, False)
+    sign(3, True, False)
     sign(1, True, False)
     sign(1, False, False)
     reps = [("rep%d" % e, 0, 3 * C, 1) for e in range(8)]
@@ -347,7 +354,7 @@ def rank_program(g, core, T, topo):
         o = ua((DRAWN_A, DRAWN_A + 1, DRAWN_A + 3)[l])
         op("V", lambda: g.vector.tensor_scalar(o[0], T.rep[:, l * C:l * C + C].indirect(T.oru[:, 0:28]), -CEN, None, ALU.add),
            reps + [("oru", 0, 28, 1)], [o[1]])
-        for dst in ((ua(0), ua(5), ub(DRAWN_B)), (ua(1), ua(2), ub(DRAWN_B + 1)), (ua(3), ub(DRAWN_B + 2)))[l]:
+        for dst in ((ua(0), ua(5), ua(4), ua(8), ub(4)), (ua(1), ua(2), ub(8), ub(7)), (ua(3), ub(3)))[l]:
             copy_unit(dst, o)
 
     tc(pw0, A("pli", 0, 28))
@@ -359,21 +366,18 @@ def rank_program(g, core, T, topo):
     tc(A("hd1", 2, 168, 6), A("c2", 0, 28))
     drawn(0)
     drawn(1)
+    drawn(2)
     sign(0, True, True)
     sign(0, False, True)
     ahead_gather(pw0, DRAWN_A, DRAWN_A + 1)
     look_up_signs(pw0)
-    for own in (True, False):
-        sign(2, own, False)
-        sign(3, own, False)
-    drawn(2)
+    sign(2, False, False)
+    sign(3, False, False)
     for b in range(4):
-        halve(b, True, b < 2)
-        halve(b, False, b < 2)
-    fill(ua(4), 0.0)
-    fill(ua(8), 0.0)
-    ahead_scan()
+        halve(b, True)
+        halve(b, False)
     wrap_signs(True)
+    ahead_scan()
 
     for s in STEP:
         last = s == STEP[-1]
@@ -389,33 +393,35 @@ def rank_program(g, core, T, topo):
         scan(A("lb", 0, C), mask, A("rb", 0, C))
         if s > 1:
             for b in range(4):
-                halve(b, True, False)
+                halve(b, True)
         ts(A("hd0", 2, 168, 6), wrapped("la"), TH, ALU.is_gt)
-        wrap_signs(False)
         ts(A("hd0", 1, 168, 6), wrapped("lb"), TH, ALU.is_gt)
         ts(A("hd1", 3, 168, 6), wrapped("lb"), TH, ALU.is_gt, float((DRAWN_A - ROT_A) * U), ALU.mult)
+        wrap_signs(False)
         ts(A("hd1", 4, 168, 6), wrapped("l2"), TH, ALU.is_le, 10.0 * U, ALU.mult)
         ts(A("hd1", 5, 168, 6), wrapped("l3"), TH, ALU.is_le, 1.0 * U, ALU.mult)
         scan(A("ho", 0, 168), A("hd0", 0, 168), A("hd1", 0, 168))
-        tc(A("f0p", 0, 28), A("ho", 5, 168, 6))
         tc(A("f0", 0, 28), A("ho", 3, 168, 6))
+        tc(A("f0p", 0, 28), A("ho", 5, 168, 6))
         f0 = A("f0", 0, 28)
-        tc(ub(0), IND(ua(0, 7), f0))
+        tc(ub(1), IND(ua(0, 7), f0))
         act(A("g1", 0, C), IND(ua(0, 18), A("f0p", 0, 28)))
-        act(ub(1), IND(ua(1, 7), f0))
-        act(ub(2), IND(ua(3, 7), f0))
-        scan(A("lp", 0, C), mask, ub(0))
+        scan(A("lp", 0, C), mask, ub(1))
         ts(A("p1", 0, 28), wrapped("lp"), SC, ALU.mult, CEN, ALU.add)
-        act(ub(3), ub(0))
-        tc(A("ra", 0, C), IND(A("g1", 0, C), A("p1", 0, 28)))
+        tc(A("ra", 0, 16 * SPL), IND(A("g1", 0, C), A("p1", 0, SPL)))
+        act(A("ra", 16 * SPL, C), IND(A("g1", 0, C), A("p1", SPL, 28)))
+        act(ub(2), IND(ua(1, 7), f0))
+        act(ub(0), IND(ua(3, 7), f0))
+        copy_unit(ub(5), ub(2))
+        copy_unit(ub(6), ub(0))
         scan(A("la", 0, C), mask, A("ra", 0, C))
         ts(A("gd0", 1, 56, 2), wrapped("la"), TG, ALU.is_gt)
         ts(A("gd1", 1, 56, 2), wrapped("la"), SC, ALU.mult, CEN, ALU.add)
         scan(A("go", 0, 56), A("gd0", 0, 56), A("gd1", 0, 56))
         f1 = A("f1", 0, 28)
         tc(f1, A("go", 1, 56, 2))
-        tc(ua(0), IND(ub(0, 5), f1))
-        act(ua(3), IND(ub(2, 5), f1))
+        tc(ua(0), IND(ub(1, 4), f1))
+        act(ua(3), IND(ub(0, 4), f1))
         scan(A("lp", 0, C), mask, ua(0))
         ts(pn, wrapped("lp"), SC, ALU.mult, CEN, ALU.add)
         rid, pid, _se = topo.addr(src)
@@ -434,23 +440,22 @@ def rank_program(g, core, T, topo):
             for b in range(4):
                 tt(A("zt", 4 * a + b, 4 * e, 4), IND(A("xh", b * C, b * C + C), ko), A("tm", b * C + a, b * C + e), ALU.add)
             quant(A("qz", a, e), A("qzs", a, e), A("zt", 4 * a, 4 * e))
-            for b in (0, 2, 1, 3):
+            for b in TO[ci]:
                 mm(bank(4 * ci + b, e - a), A("lw", 128 * b, 128 * b + 128), A("lws", 128 * b, 128 * b + 128), A("qz", a, e), A("qzs", a, e))
         if s == 1:
-            for b in range(4):
-                ts(A("eb", 512 * b + b, 512 * b + 512, 4), A("jj", 0, 128), 0.0, ALU.is_equal)
+            quant(A("qe", 0, 512), A("qes", 0, 512), A("eb", 0, 2048))
         act(A("rm", 0, C), IND(ua(3), pa))
         scan(A("lm_", 0, C), mask, A("rm", 0, C))
         ts(mw, wrapped("lm_"), SC, ALU.mult, CEN, ALU.add)
         drid, dpid, _se = topo.addr(dst)
-        md = emask(order(dst)[:8])
+        md = emask(order(dst)[8:])
         remote(lambda: g.remote_dma(T["mo%d" % s][:], T["mw%d" % s][:, 14:28], T.sem["arrm%d" % s], T.sem["locm%d" % s], dpid, drid, md),
                [mw[1]], "locm%d" % s, 8)
         arrives([("mo%d" % s, 0, 14, 1)], "arrm%d" % s, 8)
         for ci, (a, e) in enumerate(((0, CH), (CH, C))):
-            for b in ((0, 1), (2, 3, 0, 1))[ci]:
+            for b in EVS[ci]:
                 act(A("hb", b * C + a, b * C + e), bank(4 * ci + b, e - a), AF.Copy, 0.03125)
-            for b in ((2, 3), ())[ci]:
+            for b in EVV[ci]:
                 ts(A("hb", b * C + a, b * C + e), bank(4 * ci + b, e - a), 0.03125, ALU.mult)
         mf = A("mw%d" % s, 0, 14)
         for b in (0, 1):
@@ -459,55 +464,55 @@ def rank_program(g, core, T, topo):
             tc(A("hf", b, 4 * HALF, 4), IND(A("hb", b * C, b * C + C), mf))
         qf, qfs = "qf%d" % s, "qfs%d" % s
         quant(A(qf, 0, HALF), A(qfs, 0, HALF), A("hf", 0, 4 * HALF))
-        es = order(dst)
-        trs = []
-        for k in range(4):
-            trs.append((T[qf][:, 56 * k:56 * k + 56].bitcast(dt.uint8), T["ql%d" % s][:, 56 * k:56 * k + 56].bitcast(dt.uint8)))
-        trs.append((T[qfs][:], T["qls%d" % s][:]))
-        calls = [RemoteDMATransfer(dst_ids=[DstId(rid=drid, pnc=dpid)], dma_engine_mask=emask(es[2 * k:2 * k + 2]),
-                                   remote_sem=T.sem["arrq%d" % s], src=a, dst=b) for k, (a, b) in enumerate(trs)]
-        remote(lambda: g.remote_dma_fused(calls, local_sem=T.sem["locq%d" % s]), [(qf, 0, HALF, 1), (qfs, 0, HALF, 1)], "locq%d" % s, 10)
-        arrives([("ql%d" % s, 0, HALF, 1), ("qls%d" % s, 0, HALF, 1)], "arrq%d" % s, 10)
-        act(ua(1), IND(ub(1, 5), f1))
+        mq, nq = topo.mask(core, dst), len(topo.engines(core, dst))
+        remote(lambda: g.remote_dma(T["ql%d" % s][:, 0:HALF].bitcast(dt.uint8), T[qf][:, 0:HALF].bitcast(dt.uint8),
+                                    T.sem["arrq%d" % s], T.sem["locq%d" % s], dpid, drid, mq), [(qf, 0, HALF, 1)], "locq%d" % s, nq)
+        arrives([("ql%d" % s, 0, HALF, 1)], "arrq%d" % s, nq)
+        remote(lambda: g.remote_dma(T["qls%d" % s][:], T[qfs][:], T.sem["arrs%d" % s], T.sem["locs%d" % s], dpid, drid, mq),
+               [(qfs, 0, HALF, 1)], "locs%d" % s, nq)
+        arrives([("qls%d" % s, 0, HALF, 1)], "arrs%d" % s, nq)
+        act(ua(1), IND(ub(5, 4), f1))
         if not last:
             ahead_gather(pn, 0, 1)
         mo = A("mo%d" % s, 0, 14)
         for b in range(4):
             x = A("xs", 4 * HALF + b, 4 * C, 4)
             tt(x, IND(A("hb", b * C, b * C + C), mo), x, ALU.add)
-        if s == 1:
-            quant(A("qe", 0, 512), A("qes", 0, 512), A("eb", 0, 2048))
         if not last:
-            scores(True)
+            scores(True, (2, 3))
             copy_unit(ua(5), ua(0))
             copy_unit(ua(2), ua(1))
             ahead_scan()
-            sign(0, True, True)
-            for i in (1, 2, 3):
-                sign(i, True, False)
+            sign(2, True, False)
+            sign(3, True, False)
             wrap_signs(True)
         else:
             quant(A("qv", 0, 128), A("qvs", 0, 128), A("vt", 0, 512))
             quant(A("qx", HALF, C), A("qxs", HALF, C), A("xs", 4 * HALF, 4 * C))
-            mm(bank(0, HALF), A("qv", 0, 128), A("qvs", 0, 128), A("qx", HALF, C), A("qxs", HALF, C))
             for l, u in ((0, 0), (1, 1), (2, 3)):
-                ts(A("lks", l * C, l * C + C), ua(u), CEN, ALU.add)
-            act(A("ys", HALF, C), bank(0, HALF))
+                act(A("lks", l * C, l * C + C), ua(u), AF.Identity, 1.0, CEN)
             dma("Y", T.oc[:, 4 * HALF:4 * C], T.qx[:, HALF:C].bitcast(dt.uint8), [("qx", HALF, C, 1)], [])
             for k in range(4):
                 dma("Y", T.osc[4 * k:4 * k + 4, HALF:C], T.qxs[32 * k:32 * k + 4, HALF:C], [("qxs", HALF, C, 1)], [])
             dma("Y", T.lk[:], T.lks[0::16, :], [("lks", 0, 3 * C, 1)], [])
-            dma("Y", T.y[:, HALF:C], T.ys[:, HALF:C], [("ys", HALF, C, 1)], [])
         for b in range(4):
             mm(bank(4 + b, HALF), A("qe", 128 * b, 128 * b + 128), A("qes", 128 * b, 128 * b + 128),
                A("ql%d" % s, 0, HALF), A("qls%d" % s, 0, HALF))
+        if not last:
+            scores(True, (0, 1), False)
+            sign(0, True, False)
+            sign(1, True, False)
+        else:
+            mm(bank(0, HALF), A("qv", 0, 128), A("qvs", 0, 128), A("qx", HALF, C), A("qxs", HALF, C))
+            act(A("ys", HALF, C), bank(0, HALF))
+            dma("Y", T.y[:, HALF:C], T.ys[:, HALF:C], [("ys", HALF, C, 1)], [])
         for b in range(4):
             x = A("xs", b, 4 * HALF, 4)
             tt(x, bank(4 + b, HALF), x, ALU.add)
             if not last:
-                halve(b, False, False)
+                halve(b, False)
         if not last:
-            scores(False)
+            scores(False, (0, 1, 2, 3))
             sign(0, False, True)
             sign(1, False, False)
         else:

from concourse.mybir import dt, AluOpType, ActivationFunctionType

C = 448
HALF = 224
U = 448
CH = 288
STEP = [1, 2, 3]
CEN = 224.0
ROT_A, DRAWN_A = 2, 6
ROT_B, DRAWN_B = 1, 3
TO = ((0, 2, 1, 3), (0, 2, 1, 3))
EVS, EVV = ((0, 2, 1), (0, 1)), ((3,), (2, 3))
SPL = 22

SCRATCH = {
    "ps": ("psum", [128, 4096], "float32"),
    "xs": ("sbuf", [128, 4 * C], "bfloat16"),
    "xh": ("sbuf", [128, 4 * C], "bfloat16"),
    "tm": ("sbuf", [128, 4 * C], "bfloat16"),
    "zt": ("sbuf", [128, 4 * C], "bfloat16"),
    "hb": ("sbuf", [128, 4 * C], "bfloat16"),
    "hf": ("sbuf", [128, 4 * HALF], "bfloat16"),
    "qx": ("sbuf", [128, C], "float8_e4m3fn_x4"), "qxs": ("sbuf", [128, C], "uint8"),
    "qz": ("sbuf", [128, C], "float8_e4m3fn_x4"), "qzs": ("sbuf", [128, C], "uint8"),
    "ut": ("sbuf", [128, 512], "bfloat16"),
    "qu": ("sbuf", [128, 128], "float8_e4m3fn_x4"), "qus": ("sbuf", [128, 128], "uint8"),
    "qr": ("sbuf", [128, 512], "float8_e4m3fn_x4"), "qrs": ("sbuf", [128, 512], "uint8"),
    "vt": ("sbuf", [128, 512], "bfloat16"),
    "qv": ("sbuf", [128, 128], "float8_e4m3fn_x4"), "qvs": ("sbuf", [128, 128], "uint8"),
    "lw": ("sbuf", [128, 512], "float8_e4m3fn_x4"), "lws": ("sbuf", [128, 512], "uint8"),
    "eb": ("sbuf", [128, 2048], "bfloat16"),
    "qe": ("sbuf", [128, 512], "float8_e4m3fn_x4"), "qes": ("sbuf", [128, 512], "uint8"),
    "bwa": ("sbuf", [128, 18 * U], "bfloat16"),
    "bwb": ("sbuf", [128, 9 * U], "bfloat16"),
    "sg": ("sbuf", [128, 4 * C], "bfloat16"),
    "g1": ("sbuf", [128, C], "bfloat16"),
    "ra": ("sbuf", [128, C], "bfloat16"), "rb": ("sbuf", [128, C], "bfloat16"),
    "rm": ("sbuf", [128, C], "bfloat16"), "rp": ("sbuf", [128, C], "bfloat16"), "rd": ("sbuf", [128, C], "bfloat16"),
    "la": ("sbuf", [128, C], "bfloat16"), "lb": ("sbuf", [128, C], "bfloat16"),
    "l2": ("sbuf", [128, C], "bfloat16"), "l3": ("sbuf", [128, C], "bfloat16"),
    "lp": ("sbuf", [128, C], "bfloat16"), "lk_": ("sbuf", [128, C], "bfloat16"), "lm_": ("sbuf", [128, C], "bfloat16"),
    "lpp": ("sbuf", [128, C], "bfloat16"), "ldp": ("sbuf", [128, C], "bfloat16"),
    "mask": ("sbuf", [128, C], "bfloat16"), "mk2": ("sbuf", [128, C], "bfloat16"),
    "tt": ("sbuf", [128, C], "bfloat16"),
    "jj": ("sbuf", [128, 128], "float32"),
    "pi": ("sbuf", [128, 8], "int32"), "pj": ("sbuf", [128, 8], "int32"),
    "col": ("sbuf", [128, 8], "float32"),
    "cq": ("sbuf", [128, 28], "float32"), "q28": ("sbuf", [128, 28], "float32"),
    "cc": ("sbuf", [128, 28], "float32"), "c2": ("sbuf", [128, 28], "float32"),
    "ul": ("sbuf", [128, 32], "float32"), "ulu": ("sbuf", [128, 32], "uint16"),
    "oru": ("sbuf", [128, 28], "uint16"),
    "hd0": ("sbuf", [128, 168], "float32"), "hd1": ("sbuf", [128, 168], "float32"), "ho": ("sbuf", [128, 168], "float32"),
    "gd0": ("sbuf", [128, 56], "float32"), "gd1": ("sbuf", [128, 56], "float32"), "go": ("sbuf", [128, 56], "float32"),
    "ppw": ("sbuf", [128, 28], "float32"), "dpw": ("sbuf", [128, 28], "float32"),
    "f0": ("sbuf", [128, 28], "uint16"), "f0p": ("sbuf", [128, 28], "uint16"), "f1": ("sbuf", [128, 28], "uint16"),
    "p1": ("sbuf", [128, 28], "uint16"), "kw": ("sbuf", [128, 28], "uint16"),
    "pli": ("sbuf", [128, 28], "int32"),
    "rep": ("sbuf", [128, 3 * C], "int32"),
    "stage": ("dram", [8, 2, 3, C], "int32"),
    "ys": ("sbuf", [128, C], "float32"),
    "lks": ("sbuf", [128, 3 * C], "float32"),
    "pw0": ("sbuf", [128, 28], "uint16"),
}
for _r in (1, 2, 3):
    SCRATCH["pw%d" % _r] = ("sbuf", [128, 28], "uint16")
    SCRATCH["pa%d" % _r] = ("sbuf", [128, 28], "uint16")
    SCRATCH["mw%d" % _r] = ("sbuf", [128, 28], "uint16")
    SCRATCH["mo%d" % _r] = ("sbuf", [128, 14], "uint16")
    SCRATCH["qf%d" % _r] = ("sbuf", [128, HALF], "float8_e4m3fn_x4")
    SCRATCH["qfs%d" % _r] = ("sbuf", [128, HALF], "uint8")
    SCRATCH["ql%d" % _r] = ("sbuf", [128, HALF], "float8_e4m3fn_x4")
    SCRATCH["qls%d" % _r] = ("sbuf", [128, HALF], "uint8")

SEMAPHORES = ["eV", "eS", "eT", "eG"] + ["d%d" % i for i in range(60)]
for _r in (1, 2, 3):
    for _k in "pmqs":
        SEMAPHORES += ["arr%s%d" % (_k, _r), "loc%s%d" % (_k, _r)]


def make_sched(g, T):
    queues = {"V": g.vector, "S": g.scalar, "T": g.tensor, "G": g, "Y": g.sync}
    known = {q: {} for q in queues}
    count = {q: 0 for q in queues}
    total = {}
    log = {}
    ndma = [0]

    def overlap(a, b):
        if a[1] >= b[2] or b[1] >= a[2]:
            return False
        if a[3] > 1 and b[3] > 1 and a[3] == b[3] and a[1] % a[3] != b[1] % b[3]:
            return False
        return True

    def covers(a, b):
        if a[3] == 1:
            return a[1] <= b[1] and b[2] <= a[2]
        return a[3] == b[3] and a[1] % a[3] == b[1] % b[3] and a[1] <= b[1] and b[2] <= a[2]

    def wait(q, ev):
        sem, val, snap = ev
        if known[q].get(sem, 0) < val:
            queues[q].wait_ge(T.sem[sem], val)
            known[q][sem] = val
            for s, v in snap.items():
                if known[q].get(s, 0) < v:
                    known[q][s] = v

    def deps(q, reads, writes, is_async):
        need = []
        for reg, w in [(r, r[0] == "ps") for r in reads] + [(r, True) for r in writes]:
            for (old, ev, oq, oasync, owr) in log.get(reg[0], []):
                if not overlap(reg, old) or not (owr or w):
                    continue
                if oq == q and not oasync and not is_async and not owr:
                    continue
                need.append(ev)
        need.sort(key=lambda e: -e[1])
        for ev in need:
            wait(q, ev)

    def note(q, reads, writes, ev, is_async):
        for reg in reads:
            log.setdefault(reg[0], []).append((reg, ev, q, is_async, False))
        for reg in writes:
            lst = log.setdefault(reg[0], [])
            lst[:] = [e for e in lst if not covers(reg, e[0])]
            lst.append((reg, ev, q, is_async, True))

    def op(q, fn, reads, writes):
        deps(q, reads, writes, False)
        sem = "e" + q
        fn().then_inc(T.sem[sem], 1)
        count[q] += 1
        total[sem] = count[q]
        note(q, reads, writes, (sem, count[q], dict(known[q])), False)

    def dma(q, out, in_, reads, writes):
        deps(q, reads, writes, True)
        sem = "d%d" % ndma[0]
        ndma[0] += 1
        queues[q].dma_start(out, in_).then_inc(T.sem[sem], 16)
        total[sem] = 16
        note(q, reads, writes, (sem, 16, dict(known[q])), True)

    def remote(fn, reads, loc, n):
        deps("G", reads, [], True)
        fn()
        total[loc] = n
        note("G", reads, [], (loc, n, dict(known["G"])), True)

    def arrives(writes, sem, n):
        total[sem] = n
        note("far", [], writes, (sem, n, {}), True)

    def finish():
        for sem, v in total.items():
            if known["G"].get(sem, 0) < v:
                g.wait_ge(T.sem[sem], v)

    return op, dma, remote, arrives, finish


def rank_program(g, core, T, topo):
    rank = T.rank_of(core)
    if rank is None:
        return
    op, dma, remote, arrives, finish = make_sched(g, T)
    N = len(T.cores)
    ALU = AluOpType
    AF = ActivationFunctionType

    def A(name, a, b, step=1):
        t = T[name]
        return (t[:, a:b:step] if step > 1 else t[:, a:b], (name, a, b, step))

    def bank(i, n):
        return (T.ps[:, 512 * i:512 * i + n], ("ps", 512 * i, 512 * i + 512, 1))

    def IND(win, off):
        return (win[0].indirect(off[0]), win[1], off[1])

    def rr(*views):
        out = []
        for x in views:
            if isinstance(x, tuple):
                out += list(x[1:])
        return out

    def ap(x):
        return x[0] if isinstance(x, tuple) else x

    def ts(out, in0, s1, op0, s2=None, op1=None):
        if op1 is None:
            op("V", lambda: g.vector.tensor_scalar(ap(out), ap(in0), ap(s1), None, op0), rr(in0, s1), rr(out))
        else:
            op("V", lambda: g.vector.tensor_scalar(ap(out), ap(in0), ap(s1), ap(s2), op0, op1), rr(in0, s1, s2), rr(out))

    def tt(out, a, b, o):
        op("V", lambda: g.vector.tensor_tensor(ap(out), ap(a), ap(b), o), rr(a, b), rr(out))

    def tc(out, a):
        op("V", lambda: g.vector.tensor_copy(ap(out), ap(a)), rr(a), rr(out))

    def fill(out, val):
        op("V", lambda: g.vector.memset(ap(out), val), [], rr(out))

    def scan(out, d0, d1):
        op("V", lambda: g.vector.tensor_tensor_scan(ap(out), ap(d0), ap(d1), 0.0, ALU.mult, ALU.add), rr(d0, d1), rr(out))

    def act(out, a, func=AF.Copy, scale=1.0, bias=None):
        if bias is not None:
            op("S", lambda: g.scalar.activation(ap(out), ap(a), func, bias=bias, scale=scale), rr(a), rr(out))
        elif scale == 1.0:
            op("S", lambda: g.scalar.activation(ap(out), ap(a), func), rr(a), rr(out))
        else:
            op("S", lambda: g.scalar.activation(ap(out), ap(a), func, scale=scale), rr(a), rr(out))

    def iota(out, pattern, base, cm):
        op("G", lambda: g.iota(ap(out), pattern, base, cm, allow_small_or_imprecise_dtypes=True), [], rr(out))

    def quant(codes, plane, tile):
        op("V", lambda: g.vector.quantize_mx(ap(codes), ap(plane), ap(tile)), rr(tile), rr(codes, plane))

    def mm(out, w, ws, x, xs):
        op("T", lambda: g.tensor.matmul_mx(ap(out), ap(w), ap(ws), ap(x), ap(xs), True, True), rr(w, ws, x, xs), rr(out))

    def ua(i, n=1):
        return A("bwa", i * U, (i + n) * U)

    def ub(i, n=1):
        return A("bwb", i * U, (i + n) * U)

    def wrapped(name):
        return A(name, 15, C, 16)

    mask = A("mask", 0, C)
    SC, TH, TG, IF, I28, IF1 = [A("col", i, i + 1) for i in range(6)]

    def load_stage(q, l, tin, dup):
        dma(q, T.stage[:, dup, l, :], tin[:], [], [("stage", 2 * l + dup, 2 * l + dup + 1, 1)])

    dma("S", T.xs[:, 4 * HALF:4 * C], T.x[:, 4 * HALF:4 * C], [], [("xs", 4 * HALF, 4 * C, 1)])
    dma("S", T.xs[:, 0:4 * HALF], T.x[:, 0:4 * HALF], [], [("xs", 0, 4 * HALF, 1)])
    dma("Y", T.ut[:], T.u[:], [], [("ut", 0, 512, 1)])
    dma("Y", T.pli[:], T.pl[:], [], [("pli", 0, 28, 1)])
    for l, tin in ((0, T.pl), (1, T.dl), (2, T.kl)):
        load_stage("Y", l, tin, 0)
        load_stage("S", l, tin, 1)
    for e in range(8):
        dma("Y", T.rep[e::8, :], T.stage[:], [("stage", 0, 6, 1)], [("rep%d" % e, 0, 3 * C, 1)])
    dma("Y", T.lw[:].bitcast(dt.uint8), T.wc[:], [], [("lw", 0, 512, 1)])
    dma("Y", T.lws[:], T.ws[:], [], [("lws", 0, 512, 1)])
    dma("Y", T.vt[:], T.v[:], [], [("vt", 0, 512, 1)])

    iota(A("pi", 0, 1), [[1, 1]], 0, 1)
    iota(A("ul", 0, 32), [[1, 4], [16, 8]], 0, 0)
    iota(A("tt", 0, C), [[0, 28], [1, 16]], 0, 0)
    iota(A("jj", 0, 128), [[1, 128]], 0, -1)
    iota(A("q28", 0, 28), [[1, 28]], 0, 0)
    iota(A("cq", 0, 28), [[16, 28]], 0, 0)
    iota(ua(10, 8), [[0, 4], [(ROT_B - DRAWN_B) * U, 2], [0, U]], DRAWN_B * U - int(CEN), 0)
    fill(A("eb", 0, 1024), 0.0)
    act(A("eb", 1024, 2048), A("eb", 0, 1024))
    act(A("jj", 0, 128), A("jj", 0, 128), AF.Abs)
    for b in range(4):
        act(A("eb", 512 * b + b, 512 * b + 512, 4), A("jj", 0, 128), AF.Relu, -1.0, 1.0)
    ts(A("pj", 0, 1), A("pi", 0, 1), 15, ALU.bitwise_and)
    tc(IF, A("pj", 0, 1))
    tc(A("ulu", 0, 32), A("ul", 0, 32))
    ts(IF1, IF, 1.0, ALU.add)
    ts(I28, IF, 28.0, ALU.mult)
    ts(SC, IF, 15.0, ALU.is_equal, 2.0 ** -40, ALU.max)
    ts(TH, IF, 15.0, ALU.is_lt, 2.0 ** 30, ALU.mult)
    ts(TG, IF, 15.0, ALU.is_lt, 223.5 * 2.0 ** 40, ALU.mult)
    ts(TH, TH, 0.5, ALU.max)
    ts(TG, TG, 223.5, ALU.max)
    ts(A("mk2", 0, C), A("tt", 0, C), IF1, ALU.is_equal, 2.0 ** 40, ALU.mult)
    ts(mask, A("tt", 0, C), IF1, ALU.is_ge)
    ts(A("oru", 0, 28), A("q28", 0, 28), I28, ALU.add)
    tt(mask, mask, A("mk2", 0, C), ALU.max)
    ts(A("cc", 0, 28), A("cq", 0, 28), IF, ALU.add)
    quant(A("qu", 0, 128), A("qus", 0, 128), A("ut", 0, 512))
    uo = A("ulu", 0, 32)
    op("V", lambda: g.vector.tensor_copy(T.qr[:, 0:512].bitcast(dt.uint32), T.qu[:, 0:128].bitcast(dt.uint32).indirect(T.ulu[:, 0:32])),
       [("qu", 0, 128, 1), uo[1]], [("qr", 0, 512, 1)])
    op("S", lambda: g.scalar.activation(T.qrs[:, 0:512], T.qus[:, 0:128].indirect(T.ulu[:, 0:32]), AF.Copy),
       [("qus", 0, 128, 1), uo[1]], [("qrs", 0, 512, 1)])

    def scores(own, bits, q=True):
        a, b, k = (HALF, C, 0) if own else (0, HALF, 4)
        if q:
            quant(A("qx", a, b), A("qxs", a, b), A("xs", 4 * a, 4 * b))
        for i in bits:
            mm(bank(k + i, HALF), A("qr", 128 * i, 128 * i + 128), A("qrs", 128 * i, 128 * i + 128), A("qx", a, b), A("qxs", a, b))

    def sign(i, own, on_vector):
        a, k = (HALF, 0) if own else (0, 4)
        out = A("sg", i * C + a, i * C + a + HALF)
        if on_vector:
            ts(out, bank(k + i, HALF), 0.0, ALU.is_gt)
        else:
            act(out, bank(k + i, HALF), AF.Sign)

    def wrap_signs(own):
        a = HALF if own else 0
        m = A("mask", a, a + HALF)
        scan(A("l2", a, a + HALF), m, A("sg", 2 * C + a, 2 * C + a + HALF))
        scan(A("l3", a, a + HALF), m, A("sg", 3 * C + a, 3 * C + a + HALF))

    def look_up_signs(pw):
        tc(A("ra", 0, C), IND(A("sg", 0, C), pw))
        act(A("rb", 0, C), IND(A("sg", C, 2 * C), pw))

    def ahead_gather(pw, pu, du):
        act(A("rp", 0, C), IND(ua(pu), pw))
        act(A("rd", 0, C), IND(ua(du), pw))

    def ahead_scan():
        scan(A("lpp", 0, C), mask, A("rp", 0, C))
        scan(A("ldp", 0, C), mask, A("rd", 0, C))
        ts(A("ppw", 0, 28), wrapped("lpp"), SC, ALU.mult, CEN - (DRAWN_A - ROT_A) * U, ALU.add)
        ts(A("dpw", 0, 28), wrapped("ldp"), SC, ALU.mult, CEN, ALU.add)
        tt(A("hd1", 1, 168, 6), A("dpw", 0, 28), A("c2", 0, 28), ALU.subtract)
        tt(A("hd1", 0, 168, 6), A("ppw", 0, 28), A("dpw", 0, 28), ALU.subtract)

    def halve(b, own):
        a = HALF if own else 0
        act(A("xh", b * C + a, b * C + a + HALF), A("xs", 4 * a + b, 4 * a + 4 * HALF, 4), AF.Copy, 0.5)

    def copy_unit(dst, src):
        dma("Y", dst[0], src[0], [src[1]], [dst[1]])

    def order(to):
        e = topo.engines(core, to)
        return e[::2] + e[1::2]

    def emask(es):
        m = 0
        for e in es:
            m |= 1 << e
        return m

    pw0 = A("pw0", 0, 28)
    scores(True, (2, 3, 0, 1))
    scores(False, (0, 1, 2, 3))
    sign(2, True, False)
    sign(3, True, False)
    sign(1, True, False)
    sign(1, False, False)
    reps = [("rep%d" % e, 0, 3 * C, 1) for e in range(8)]

    def drawn(l):
        o = ua((DRAWN_A, DRAWN_A + 1, DRAWN_A + 3)[l])
        op("V", lambda: g.vector.tensor_scalar(o[0], T.rep[:, l * C:l * C + C].indirect(T.oru[:, 0:28]), -CEN, None, ALU.add),
           reps + [("oru", 0, 28, 1)], [o[1]])
        for dst in ((ua(0), ua(5), ua(4), ua(8), ub(4)), (ua(1), ua(2), ub(8), ub(7)), (ua(3), ub(3)))[l]:
            copy_unit(dst, o)

    tc(pw0, A("pli", 0, 28))
    fill(A("hd0", 0, 168), 1.0)
    ts(A("c2", 0, 28), A("cc", 0, 28), float(ROT_A * U), ALU.add)
    ts(A("gd0", 0, 56, 2), A("cc", 0, 28), 0.0, ALU.mult)
    tc(A("gd1", 0, 56, 2), A("cc", 0, 28))
    ts(A("hd0", 0, 168, 6), A("cc", 0, 28), 0.0, ALU.mult)
    tc(A("hd1", 2, 168, 6), A("c2", 0, 28))
    drawn(0)
    drawn(1)
    drawn(2)
    sign(0, True, True)
    sign(0, False, True)
    ahead_gather(pw0, DRAWN_A, DRAWN_A + 1)
    look_up_signs(pw0)
    sign(2, False, False)
    sign(3, False, False)
    for b in range(4):
        halve(b, True)
        halve(b, False)
    wrap_signs(True)
    ahead_scan()

    for s in STEP:
        last = s == STEP[-1]
        src, dst = T.cores[(rank - s) % N], T.cores[(rank + s) % N]
        pw = A("pw%d" % (s - 1), 0, 28)
        pn, pa, mw = A("pw%d" % s, 0, 28), A("pa%d" % s, 0, 28), A("mw%d" % s, 0, 28)

        if s > 1:
            look_up_signs(pw)
            sign(2, False, False)
            sign(3, False, False)
        scan(A("la", 0, C), mask, A("ra", 0, C))
        scan(A("lb", 0, C), mask, A("rb", 0, C))
        if s > 1:
            for b in range(4):
                halve(b, True)
        ts(A("hd0", 2, 168, 6), wrapped("la"), TH, ALU.is_gt)
        ts(A("hd0", 1, 168, 6), wrapped("lb"), TH, ALU.is_gt)
        ts(A("hd1", 3, 168, 6), wrapped("lb"), TH, ALU.is_gt, float((DRAWN_A - ROT_A) * U), ALU.mult)
        wrap_signs(False)
        ts(A("hd1", 4, 168, 6), wrapped("l2"), TH, ALU.is_le, 10.0 * U, ALU.mult)
        ts(A("hd1", 5, 168, 6), wrapped("l3"), TH, ALU.is_le, 1.0 * U, ALU.mult)
        scan(A("ho", 0, 168), A("hd0", 0, 168), A("hd1", 0, 168))
        tc(A("f0", 0, 28), A("ho", 3, 168, 6))
        tc(A("f0p", 0, 28), A("ho", 5, 168, 6))
        f0 = A("f0", 0, 28)
        tc(ub(1), IND(ua(0, 7), f0))
        act(A("g1", 0, C), IND(ua(0, 18), A("f0p", 0, 28)))
        scan(A("lp", 0, C), mask, ub(1))
        ts(A("p1", 0, 28), wrapped("lp"), SC, ALU.mult, CEN, ALU.add)
        tc(A("ra", 0, 16 * SPL), IND(A("g1", 0, C), A("p1", 0, SPL)))
        act(A("ra", 16 * SPL, C), IND(A("g1", 0, C), A("p1", SPL, 28)))
        act(ub(2), IND(ua(1, 7), f0))
        act(ub(0), IND(ua(3, 7), f0))
        copy_unit(ub(5), ub(2))
        copy_unit(ub(6), ub(0))
        scan(A("la", 0, C), mask, A("ra", 0, C))
        ts(A("gd0", 1, 56, 2), wrapped("la"), TG, ALU.is_gt)
        ts(A("gd1", 1, 56, 2), wrapped("la"), SC, ALU.mult, CEN, ALU.add)
        scan(A("go", 0, 56), A("gd0", 0, 56), A("gd1", 0, 56))
        f1 = A("f1", 0, 28)
        tc(f1, A("go", 1, 56, 2))
        tc(ua(0), IND(ub(1, 4), f1))
        act(ua(3), IND(ub(0, 4), f1))
        scan(A("lp", 0, C), mask, ua(0))
        ts(pn, wrapped("lp"), SC, ALU.mult, CEN, ALU.add)
        rid, pid, _se = topo.addr(src)
        m = emask(order(src)[:8])
        remote(lambda: g.remote_dma(T["pa%d" % s][:], T["pw%d" % s][:], T.sem["arrp%d" % s], T.sem["locp%d" % s], pid, rid, m),
               [pn[1]], "locp%d" % s, 8)
        arrives([pa[1]], "arrp%d" % s, 8)
        kw = A("kw", 0, 28)
        scan(A("lk_", 0, C), mask, ua(3))
        ts(kw, wrapped("lk_"), SC, ALU.mult, CEN, ALU.add)
        for ci, (a, e) in enumerate(((0, CH), (CH, C))):
            po = A("pw%d" % s, a // 16, e // 16)
            ko = A("kw", a // 16, e // 16)
            for b in range(4):
                act(A("tm", b * C + a, b * C + e), IND(A("xh", b * C, b * C + C), po))
            for b in range(4):
                tt(A("zt", 4 * a + b, 4 * e, 4), IND(A("xh", b * C, b * C + C), ko), A("tm", b * C + a, b * C + e), ALU.add)
            quant(A("qz", a, e), A("qzs", a, e), A("zt", 4 * a, 4 * e))
            for b in TO[ci]:
                mm(bank(4 * ci + b, e - a), A("lw", 128 * b, 128 * b + 128), A("lws", 128 * b, 128 * b + 128), A("qz", a, e), A("qzs", a, e))
        if s == 1:
            quant(A("qe", 0, 512), A("qes", 0, 512), A("eb", 0, 2048))
        act(A("rm", 0, C), IND(ua(3), pa))
        scan(A("lm_", 0, C), mask, A("rm", 0, C))
        ts(mw, wrapped("lm_"), SC, ALU.mult, CEN, ALU.add)
        drid, dpid, _se = topo.addr(dst)
        md = emask(order(dst)[8:])
        remote(lambda: g.remote_dma(T["mo%d" % s][:], T["mw%d" % s][:, 14:28], T.sem["arrm%d" % s], T.sem["locm%d" % s], dpid, drid, md),
               [mw[1]], "locm%d" % s, 8)
        arrives([("mo%d" % s, 0, 14, 1)], "arrm%d" % s, 8)
        for ci, (a, e) in enumerate(((0, CH), (CH, C))):
            for b in EVS[ci]:
                act(A("hb", b * C + a, b * C + e), bank(4 * ci + b, e - a), AF.Copy, 0.03125)
            for b in EVV[ci]:
                ts(A("hb", b * C + a, b * C + e), bank(4 * ci + b, e - a), 0.03125, ALU.mult)
        mf = A("mw%d" % s, 0, 14)
        for b in (0, 1):
            act(A("hf", b, 4 * HALF, 4), IND(A("hb", b * C, b * C + C), mf))
        for b in (2, 3):
            tc(A("hf", b, 4 * HALF, 4), IND(A("hb", b * C, b * C + C), mf))
        qf, qfs = "qf%d" % s, "qfs%d" % s
        quant(A(qf, 0, HALF), A(qfs, 0, HALF), A("hf", 0, 4 * HALF))
        mq, nq = topo.mask(core, dst), len(topo.engines(core, dst))
        remote(lambda: g.remote_dma(T["ql%d" % s][:, 0:HALF].bitcast(dt.uint8), T[qf][:, 0:HALF].bitcast(dt.uint8),
                                    T.sem["arrq%d" % s], T.sem["locq%d" % s], dpid, drid, mq), [(qf, 0, HALF, 1)], "locq%d" % s, nq)
        arrives([("ql%d" % s, 0, HALF, 1)], "arrq%d" % s, nq)
        remote(lambda: g.remote_dma(T["qls%d" % s][:], T[qfs][:], T.sem["arrs%d" % s], T.sem["locs%d" % s], dpid, drid, mq),
               [(qfs, 0, HALF, 1)], "locs%d" % s, nq)
        arrives([("qls%d" % s, 0, HALF, 1)], "arrs%d" % s, nq)
        act(ua(1), IND(ub(5, 4), f1))
        if not last:
            ahead_gather(pn, 0, 1)
        mo = A("mo%d" % s, 0, 14)
        for b in range(4):
            x = A("xs", 4 * HALF + b, 4 * C, 4)
            tt(x, IND(A("hb", b * C, b * C + C), mo), x, ALU.add)
        if not last:
            scores(True, (2, 3))
            copy_unit(ua(5), ua(0))
            copy_unit(ua(2), ua(1))
            ahead_scan()
            sign(2, True, False)
            sign(3, True, False)
            wrap_signs(True)
        else:
            quant(A("qv", 0, 128), A("qvs", 0, 128), A("vt", 0, 512))
            quant(A("qx", HALF, C), A("qxs", HALF, C), A("xs", 4 * HALF, 4 * C))
            for l, u in ((0, 0), (1, 1), (2, 3)):
                act(A("lks", l * C, l * C + C), ua(u), AF.Identity, 1.0, CEN)
            dma("Y", T.oc[:, 4 * HALF:4 * C], T.qx[:, HALF:C].bitcast(dt.uint8), [("qx", HALF, C, 1)], [])
            for k in range(4):
                dma("Y", T.osc[4 * k:4 * k + 4, HALF:C], T.qxs[32 * k:32 * k + 4, HALF:C], [("qxs", HALF, C, 1)], [])
            dma("Y", T.lk[:], T.lks[0::16, :], [("lks", 0, 3 * C, 1)], [])
        for b in range(4):
            mm(bank(4 + b, HALF), A("qe", 128 * b, 128 * b + 128), A("qes", 128 * b, 128 * b + 128),
               A("ql%d" % s, 0, HALF), A("qls%d" % s, 0, HALF))
        if not last:
            scores(True, (0, 1), False)
            sign(0, True, False)
            sign(1, True, False)
        else:
            mm(bank(0, HALF), A("qv", 0, 128), A("qvs", 0, 128), A("qx", HALF, C), A("qxs", HALF, C))
            act(A("ys", HALF, C), bank(0, HALF))
            dma("Y", T.y[:, HALF:C], T.ys[:, HALF:C], [("ys", HALF, C, 1)], [])
        for b in range(4):
            x = A("xs", b, 4 * HALF, 4)
            tt(x, bank(4 + b, HALF), x, ALU.add)
            if not last:
                halve(b, False)
        if not last:
            scores(False, (0, 1, 2, 3))
            sign(0, False, True)
            sign(1, False, False)
        else:
            quant(A("qx", 0, HALF), A("qxs", 0, HALF), A("xs", 0, 4 * HALF))
            mm(bank(1, HALF), A("qv", 0, 128), A("qvs", 0, 128), A("qx", 0, HALF), A("qxs", 0, HALF))
            dma("Y", T.oc[:, 0:4 * HALF], T.qx[:, 0:HALF].bitcast(dt.uint8), [("qx", 0, HALF, 1)], [])
            for k in range(4):
                dma("YS"[k % 2], T.osc[4 * k:4 * k + 4, 0:HALF], T.qxs[32 * k:32 * k + 4, 0:HALF], [("qxs", 0, HALF, 1)], [])
            tc(A("ys", 0, HALF), bank(1, HALF))
            dma("S", T.y[:, 0:HALF], T.ys[:, 0:HALF], [("ys", 0, HALF, 1)], [])
    finish()
